import numpy as np, ml_dtypes
CORES = [5,29,101,125,133,157,229,253]
N = 8
import mx_ref
BF = ml_dtypes.bfloat16
def gcols(t, e):
    v = np.concatenate([t.reshape(8, 16, -1, 4), np.zeros((8, 16, 1, 4), BF)], axis=2)
    return np.ascontiguousarray(np.stack([v[g][:, e[g]] for g in range(8)])).reshape(128, -1)
def tile(rs):
    return np.stack(rs, axis=2).reshape(128, -1).astype(BF)
def pick(q, e):
    c = np.concatenate([q[0].reshape(128, -1, 4), np.zeros((128, 1, 4), np.uint8)], axis=1); s = np.concatenate([q[1], np.ones((16, 1), np.uint8)], axis=1)
    return (np.ascontiguousarray(c[:, e].reshape(128, -1)), np.ascontiguousarray(s[:, e]))
def join(*qs):
    return (np.concatenate([q[0] for q in qs], axis=1), np.concatenate([q[1] for q in qs], axis=1))
def put(q, e, v):
    c, s = q[0].reshape(128, -1, 4).copy(), q[1].copy(); c[:, e] = v[0].reshape(128, -1, 4); s[:, e] = v[1]
    return (c.reshape(128, -1), s)
def pk(c, s):
    return (np.ascontiguousarray(c), mx_ref.live(s))
def emit(q):
    return q[0], q[1]
def packed(v, rng):
    q = [mx_ref.quantize(np.ascontiguousarray(v[r])) for r in range(N)]
    return np.stack([a for a, b in q]), np.stack([mx_ref.plane(b, rng) for a, b in q])
def values_of_codes():
    e, c = np.zeros((128, 128, 4), np.float32), np.zeros((128, 2, 4), np.uint8)
    e[np.arange(128), np.arange(128), 0] = 1
    c[:127, :, 0] = np.arange(256).reshape(2, 128).T[:127]
    return mx_ref.matmul(mx_ref.quantize(e.reshape(128, 512).astype(BF)), (c.reshape(128, 8), np.full((16, 2), 127, np.uint8))).T.reshape(-1).astype(np.float64)
CODE_VALUE, SCALE_VALUE = values_of_codes(), 2.0 ** (np.arange(256) - 127.0)
def decode(q):
    return (CODE_VALUE[q[0]].reshape(16, 8, -1, 4) * SCALE_VALUE[q[1]][:, None, :, None] + 0.0).reshape(128, -1).astype(np.float32)
def f(rng, *shape):
    return mx_ref.flush((rng.standard_normal(shape, dtype=np.float32) * np.exp2(rng.integers(-2, 3, shape[:-1] + (1,)))).astype(BF))
def wide(rng, *shape, cols=0):
    v = rng.standard_normal(shape, dtype=np.float32) * np.exp2(rng.integers(-12, 13, shape)).astype(np.float32)
    if cols: v *= np.repeat(np.exp2(rng.integers(-cols, cols + 1, shape[:-2] + (1, shape[-1] // 4))) * (rng.random(shape[:-2] + (1, shape[-1] // 4)) > 0.0625), 4, axis=-1).astype(np.float32)
    return mx_ref.flush(v.astype(BF))
C, P, R = 256, 64, 2
def big(v):
    v = v.astype(np.float32)
    v[np.abs(v) < np.float32(2.0 ** -16)] = 0
    return v.astype(BF)
def numbers_of(rng):
    return {"x": big(f(rng, N, 128, 4 * C)), "u": np.array(f(rng, N, 128, 512)), "v": np.array(f(rng, N, 128, 512))}
def layers(rng):
    return big(f(rng, N, 128, 2048)).reshape(N, 8, 16, 4, 8, 16, 4)
def weights(rng, w):
    c, p = packed(np.ascontiguousarray(w).reshape(N, 128, 2048), rng)
    return {"wc": c, "ws": p}
def setup_inputs(rng):
    return {**numbers_of(rng), **weights(rng, layers(rng))}
def setup_inputs_ties(rng):
    d = numbers_of(rng)
    e = rng.permutation(N)
    x = d["x"].reshape(N, 8, 16, C, 4)
    for r in range(N):
        k = rng.permutation(C) % 3
        if r == e[0]: k = np.zeros(C, int)
        elif r in e[2::2]: k = rng.permutation(3)[np.arange(C) % 3]
        a = x[r][:, :8, :3].copy()
        a[:, :, 2] = 0
        x[r][:, :8] = a[:, :, k]
    x[e[1]] = 0
    u = d["u"].reshape(N, 8, 16, 128, 4)
    for i in range(5): u[:, :, 8:, i::16] = 0
    w = layers(rng)
    w[:, :, :, :, :, :8] = 0
    return {"x": x.reshape(N, 128, 4 * C), "u": u.reshape(N, 128, 512), "v": d["v"], **weights(rng, w)}
def setup_inputs_near(rng):
    d = numbers_of(rng)
    x = d["x"].astype(np.float32).reshape(N, 8, 16, C, 4)
    x[:, :, :9] = 0
    u = d["u"].reshape(N, 128, 128, 4)
    for i in range(5): u[:, :, i::16] = 0
    o = rng.permutation(N) % 4
    for r in range(N):
        k = 2.0 ** -30 if o[r] else 1.0
        c = rng.integers(0, 2, (8, 1)) * 2.0 - 1.0
        s = rng.integers(-1, 2, (8, C, 4))
        if o[r] < 2:
            n = rng.integers(0, 16, (8, C))
            x[r, :, 0] = ((n[:, :, None] >> np.arange(4)) & 1) * np.exp2(np.arange(4) - 23.0)
            x[r, :, 1, :, 0] = 2.0 ** -10
            x[r, :, 2] = s * 2.0 ** -10
            x[r, :, 8, :, 0] = c
        else:
            x[r, :, 0, :, 0] = c * rng.integers(1, 16, (8, C)) * 2.0 ** -29
            x[r, :, 2] = s * 2.0 ** -29
        for g in rng.permutation(8)[:4]: x[r, g, 8 if o[r] < 2 else 0, rng.integers(C), 0] = 2.0 ** 29 * (rng.integers(0, 2) * 2.0 - 1.0)
        for h in range(0, 128, 16):
            u[r, h, h + 4] = k
            u[r, h + 1, h + 4, 0] = k
            u[r, h + 8, h + 4, 0] = k
            for i in range(4): u[r, h + 2, h + i, i] = k
    w = layers(rng)
    w[:, :, :9] = 0
    w[:, :, :, :, :, :9] = 0
    return {"x": x.reshape(N, 128, 4 * C).astype(BF), "u": u.reshape(N, 128, 512), "v": d["v"], **weights(rng, w)}
def setup_inputs_skew(rng):
    d = numbers_of(rng)
    x = d["x"].astype(np.float32).reshape(N, 8, 16, C, 4)
    t = (1 + (2 * rng.integers(0, 64, (N, 8, 8, C // 2, 4)) + 1) / 128) * np.exp2(-rng.integers(8, 15, (N, 8, 8, C // 2, 4)).astype(float)) * (rng.integers(0, 2, (N, 8, 8, C // 2, 4)) * 2.0 - 1.0)
    t[:, :, 3, :, 1] = 1.96875
    x[:, :, 8:, ::2] = t * np.exp2(rng.integers(-2, 3, (N, 8, 1, C // 2, 1)).astype(float))
    u = d["u"].reshape(N, 128, 128, 4)
    for i in range(5): u[:, :, i::16] = 0
    for h in range(0, 128, 16):
        for b in range(12): u[:, h + b // 4, h + 4, b % 4] = 2.0 ** b
        for i in range(4): u[:, h + 3, h + i, i] = 1
    n = -(-C // 7)
    n2 = n - (-(C - n) // 5)
    n3 = n2 - (-(C - n2) // 3)
    down = C - 1 - np.arange(C)
    for r in range(N):
        for j, g in enumerate(rng.permutation(8)):
            a = np.append(rng.permutation(np.delete(np.arange(4), j % 4)), j % 4)
            two = np.zeros((C, 4), int)
            if j < 6:
                two[:n, a[0]] = 1
                two[n:n2, a[1]] = 1
            if j < 4: two[n2:n3, a[2]] = 1
            if j >= 6: two[-(-2 * C // 5):] = 1
            o = rng.permutation(C)
            x[r, g][:3, o] = (down[None, :, None] >> (4 * np.arange(3)[:, None, None] + np.arange(4))) & 1
            x[r, g][3, o] = np.where(two > 0, 1, -rng.integers(0, 2, (C, 4)))
    w = layers(rng)
    w[:, :, :, :, :, :4] = 0
    return {"x": x.reshape(N, 128, 4 * C).astype(BF), "u": u.reshape(N, 128, 512), "v": d["v"], **weights(rng, w)}
def setup_inputs_huge(rng):
    d = numbers_of(rng)
    o = rng.permutation(N)
    h = rng.permutation(8)
    x = -0.95 - 0.05 * rng.random((N, 8, 16, C, 4))
    x[:, h[4:]] = (0.75 + 0.1 * rng.random((N, 4, 16, C, 4))) * rng.choice([-1.0, 1.0], (N, 4, 1, C, 1))
    u = d["u"].reshape(N, 128, 128, 4)
    for i in range(5): u[:, :, i::16] = 0
    for r in range(N):
        if o[r] < N // 2: x[r] = (0.8 + 0.1 * rng.random((8, 16, C, 4))) * rng.choice([-1.0, 1.0], (1, 1, C, 1))
        for g in range(8):
            for i in range(5):
                a, n = 16 * int(rng.choice(h[4:])), 16
                if i == 4 and o[r] < N // 2: a, n = 0, 128
                u[r, a:a + n, 16 * g + i] = (2.0 ** 30 * (1 - 0.05 * rng.random((n, 4))) * rng.choice([-1.0, 1.0])).astype(np.float32).astype(BF)
    w = np.zeros((N, 128, 4, 128, 4), np.float32)
    i = np.arange(128)
    for b in range(4): w[:, i, b, i, b] = -1
    return {"x": (2.0 ** 30 * x).astype(np.float32).reshape(N, 128, 4 * C).astype(BF), "u": u.reshape(N, 128, 512), "v": d["v"], **weights(rng, w.astype(BF))}
def setup_inputs_spread(rng):
    d = setup_inputs(rng)
    d["x"] = big(wide(rng, N, 128, 4 * C, cols=6))
    return d
def check_inputs(d):
    b = []
    for k in ("x", "u", "v"):
        a = np.abs(d[k].astype(np.float32))
        if not (np.isfinite(a).all() and ((a == 0) | (a >= 2.0 ** -30) & (a <= 2.0 ** 30)).all()): b.append("a value of " + k)
    none, least, most = [emit(mx_ref.quantize(np.full((128, 16), k, np.float32).astype(BF)))[1][0, 0] for k in (0.0, 2.0 ** -30, 2.0 ** 30)]
    for r in range(N):
        if ((d["wc"][r] == 0x7F) | (d["wc"][r] == 0xFF)).any(): b.append("wc: a code that is no number")
        s = mx_ref.live(d["ws"][r])
        if ((s != none) & ((s < least) | (s > most))).any(): b.append("ws: a scale out of range")
    return b
def divide(sums):
    g = np.arange(8)
    first, end = np.zeros((4, 8), np.int64), np.full((4, 8), C)
    a, left = np.zeros(8, np.int64), np.ones((4, 8), bool)
    for m in (4, 3, 2):
        worth = sums - np.stack([sums[k, g, a] for k in range(4)])[:, :, None]
        e = np.sum(m * worth < worth[:, :, -1:], axis=2)
        e[~left] = C + 1
        k = np.argmin(e, axis=0)
        first[k, g] = a
        a = e[k, g]
        end[k, g] = a
        left[k, g] = False
    first[np.argmax(left, axis=0), g] = a
    return first, end
def reference(x, u, v, wc, ws):
    qu = [mx_ref.quantize(u[r]) for r in range(N)]
    lay = [pk(wc[r], ws[r]) for r in range(N)]
    now = [x[r] for r in range(N)]
    of = [np.arange(k * P, k * P + P) for k in range(4)]
    slot_of = np.zeros((N, 8, C), np.int64)
    for t in range(R):
        sent, best, made = [], [], []
        slot_of[:] = -1
        for r in range(N):
            s = mx_ref.matmul(qu[r], mx_ref.quantize(now[r])) + np.float32(0.0)
            o = np.argsort(-s[4::16], axis=1, kind="stable")
            worth = np.stack([1 + (np.take_along_axis(s[k::16], o, axis=1) > 0) for k in range(4)])
            first, end = divide(np.concatenate([np.zeros((4, 8, 1), np.int64), np.cumsum(worth, axis=2)], axis=2))
            slots = []
            for k in range(4):
                i = first[k][:, None] + np.arange(P)
                slots.append(np.where(i < end[k][:, None], np.take_along_axis(o, np.minimum(i, C - 1), axis=1), -1))
            slots = np.concatenate(slots, axis=1)
            for g in range(8):
                j = np.nonzero(slots[g] >= 0)[0]
                slot_of[r, g, slots[g, j]] = j
            sent.append(mx_ref.quantize(gcols(now[r], slots)))
            best.append(gcols(now[r], o[:, :P]))
        for r in range(N):
            came = decode(join(*[pick(sent[(r - k) % N], of[k]) for k in range(4)]))
            z = mx_ref.quantize(((came + np.tile(best[r].astype(np.float32), (1, 4))) * np.float32(0.5)).astype(BF))
            made.append(mx_ref.quantize(tile([mx_ref.matmul(pick(lay[r], np.arange(128 * b, 128 * b + 128)), z) * np.float32(0.03125) for b in range(4)])))
        for r in range(N):
            back = decode(join(*[pick(made[(r + k) % N], of[k]) for k in range(4)])).astype(BF)
            now[r] = (now[r].astype(np.float32) + gcols(back, slot_of[r]).astype(np.float32)).astype(BF)
    y, sl = np.zeros((N, 128, C), np.float32), np.zeros((N, 8, C), np.float32)
    oc, osc = np.zeros((N, 128, 4 * C), np.uint8), np.zeros((N, 16, C), np.uint8)
    for r in range(N):
        q = mx_ref.quantize(now[r])
        y[r] = mx_ref.matmul(mx_ref.quantize(v[r]), q)
        sl[r] = slot_of[r]
        oc[r], osc[r] = emit(q)
    return {"y": y, "sl": sl, "oc": oc, "osc": osc}

@@ -1,0 +1,520 @@
+from concourse.bass import DstId, RemoteDMATransfer
+from concourse.mybir import dt, AluOpType as A, AxisListType, ActivationFunctionType as F
+
+N = 8
+BIG = float(2.0 ** 90)
+PT = 336
+NO = 320
+PD = 272
+WD = (128, 128, 192, 256)
+SCRATCH = {}
+PLACE = {}
+PSUM = ("pr", "pd")
+
+
+def _decl():
+    f, b, i, h, q, s = "float32", "bfloat16", "int32", "uint16", "float8_e4m3fn_x4", "uint8"
+
+    def add(names, n, d, where="sbuf"):
+        for k in names.split():
+            SCRATCH[k] = (where, [128, n], d)
+            PLACE[k] = (k, 0, n)
+
+    def share(buf, d, *groups):
+        at = 0
+        for names, n in groups:
+            for k in names.split():
+                PLACE[k] = (buf, at, n)
+                at += -(-n // 32) * 32
+        SCRATCH[buf] = ("sbuf", [128, at], d)
+    add("pr pd", 2048, f, "psum")
+    add("ub vb", 512, b)
+    add("qu qv", 128, q), add("su sv", 128, s)
+    add("qu2", 256, q), add("su2", 256, s)
+    add("wq", 512, q), add("wsc", 512, s)
+    share("ci", i, ("iD dl", 256), ("iC", 512), ("iL", 8), ("iP pq pc pg", 2), ("iS", 16))
+    share("cfl", f, ("fI maskb d0 ones io20 kk01 bigt", 256), ("ek", 2056), ("tb", 264), ("cf ch ca1 ca2 ca3 kf kc0 pgf gpf", 2), ("s16p c16 k16", 16))
+    add("ul", 16, h)
+    add("gt", 512, b), add("hf ex", 516, b)
+    share("qk", q, ("qg qe0 qe1 qe2 qe3", 128)), share("sk", s, ("sg se0 se1 se2 se3", 128))
+    for k in range(4):
+        add("cm%d" % k, 4 * WD[k], b)
+    add("cme", 1024, b)
+    share("qc", q, ("qc0 qc1", 128), ("qc2", 192), ("qc3 qce", 256)), share("sc", s, ("sc0 sc1", 128), ("sc2", 192), ("sc3 sce", 256))
+    add("dd ow sg1 sg2 pay dw2 ow2 win cum dw3 ow3 ycp slr", 256, f), add("junk", 1920, b), add("junk2", 768, b)
+    add("rl13 rl14 rl15", 256, b)
+    share("sm", f, ("rs rt rk ck1 ck2 ck3 bs2 bs3 bt io w1 w2 w3 xa xb t1 t2 t3 en vl plf c1 c2 c3 z1 z2 z3 y1 y2 y3 sv1 rl sf", 16),
+          ("tm ac1 ac2 ac3 km1 km2 km3 kx1 kx2 kcb kcc fr1 fr2 fr3 dda em af1 af2 af3 cb1 cb2 cb3 cb4 db2 db3 db4 da2 da3 e1 e2", 2))
+    share("li", h, ("ro pl so ol", 16), ("ky1 ky2 ky3 ao1 ao2 ao3", 2))
+    add("xp", 1024, b), add("xs", 4 * PT, b), add("e2x", 512, b), add("dwn", 4 * PD, b)
+    add("b13 b02 za zb ha hb", 512, b), add("qza qzb", 128, q), add("sza szb", 128, s)
+    for t in range(3):
+        add("xi%d" % t, 1024, b), add("qx%d" % t, 256, q), add("sx%d" % t, 256, s)
+    for t in range(2):
+        add("qb%d lbc%d lhc%d qh%d" % ((t,) * 4), 128, q)
+        add("sb%d lbs%d lhs%d sh%d" % ((t,) * 4), 128, s)
+        add("wbc%d whc%d" % (t, t), 192, q), add("wbs%d whs%d" % (t, t), 192, s)
+        add("rbc%d rhc%d" % (t, t), 64, q), add("rbs%d rhs%d" % (t, t), 64, s)
+
+
+_decl()
+SEMAPHORES = ["ev", "es", "et", "eg", "loc"] + ["d%d" % k for k in range(14)] + [
+    "%s%s%d" % (a, b, t) for a in ("rc", "rs", "ao", "ad") for b in "bh" for t in range(2)]
+
+
+def _relays(topo, cores, r):
+    c = cores[r]
+    own = [d for d in topo.cores_of(c) if d != c and topo.may_write(d, cores[(r + 1) % N]) and topo.may_write(d, cores[(r + 3) % N])]
+    near, far = [[d for d in own if (topo.die(d) == topo.die(c)) == same] for same in (True, False)]
+    return [(near[0], "c", 0), (near[-1], "s", 0), (far[0], "c", 1), (far[-1], "s", 1)]
+
+
+def _mask(engines):
+    return sum(1 << int(e) for e in engines)
+
+
+def _relay(g, core, T, topo, r, w, i):
+    n = 0
+    for t in range(2):
+        for ph in "bh":
+            k = 2 * i + 1
+            dst = T.cores[(r + (k if ph == "b" else -k)) % N]
+            rid, pid = topo.addr(dst, core)
+            en = topo.engines(core, dst)
+            g.wait_ge(T.sem["r%s%s%d" % (w, ph, t)], 8)
+            src, d = T["r%s%s%d" % (ph, w, t)][:, 0:64], T["l%s%s%d" % (ph, w, t)][:, 64 * i:64 * i + 64]
+            if w == "c":
+                src, d = src.bitcast(dt.uint8), d.bitcast(dt.uint8)
+            g.remote_dma(out_ap=d, in_ap=src, remote_sem=T.sem["ao%s%d" % (ph, t)], local_sem=T.sem.loc, pid=pid, routing_id=rid,
+                         dma_engine_mask=_mask(en))
+            n += len(en)
+    g.wait_ge(T.sem.loc, n)
+
+
+def rank_program(g, core, T, topo):
+    rank = T.rank_of(core)
+    if rank is None:
+        for r in range(N):
+            if core in topo.cores_of(T.cores[r]):
+                for d, w, i in _relays(topo, T.cores, r):
+                    if d == core:
+                        _relay(g, core, T, topo, r, w, i)
+        return
+    eng = {"v": g.vector, "s": g.scalar, "t": g.tensor, "g": g, "y": g.sync}
+    seen = {q: {} for q in eng}
+    tot, snap, acc, nd = {}, {}, {}, [0]
+
+    def R(n, lo=0, hi=None, st=1):
+        buf, at, w = PLACE[n]
+        return (buf, at + lo, at + (w if hi is None else hi), st)
+
+    def ap(r):
+        n, lo, hi, st = r
+        return T[n][:, lo:hi] if st == 1 else T[n][:, lo:hi:st]
+
+    def meet(a, b):
+        if a[0] in PSUM:
+            return a[1] // 512 <= (b[2] - 1) // 512 and b[1] // 512 <= (a[2] - 1) // 512
+        if a[1] >= b[2] or b[1] >= a[2]:
+            return False
+        return not (a[3] == b[3] and a[3] > 1 and (a[1] - b[1]) % a[3])
+
+    def wait(q, sem, val):
+        if seen[q].get(sem, 0) >= val:
+            return
+        eng[q].wait_ge(T.sem[sem], val)
+        seen[q][sem] = val
+        for k, v in snap.get((sem, val), {}).items():
+            seen[q][k] = max(seen[q].get(k, 0), v)
+
+    def before(q, outs, ins, own, open_=False):
+        need = {}
+        for r, wr in [(r, True) for r in outs] + [(r, False) for r in ins]:
+            for o, ow, sem, val, oq in acc.get(r[0], ()):
+                if not (wr or ow or (r[0] in PSUM and oq != own)) or not meet(r, o):
+                    continue
+                if oq == own == "t" and open_:
+                    continue
+                need[sem] = max(need.get(sem, 0), val)
+        for sem in sorted(need):
+            wait(q, sem, need[sem])
+
+    def after(q, outs, ins, sem, val, own):
+        snap[(sem, val)] = dict(seen[q])
+        for r in outs:
+            l = acc.setdefault(r[0], [])
+            if r[3] == 1 and r[0] not in PSUM:
+                l[:] = [e for e in l if not (e[0][1] >= r[1] and e[0][2] <= r[2])]
+            l.append((r, True, sem, val, own))
+        for r in ins:
+            acc.setdefault(r[0], []).append((r, False, sem, val, own))
+
+    def op(q, outs, ins, call, open_=False):
+        before(q, outs, ins, q, open_)
+        sem = "e" + q
+        tot[sem] = tot.get(sem, 0) + 1
+        call(eng[q]).then_inc(T.sem[sem], 1)
+        after(q, outs, ins, sem, tot[sem], q)
+
+    def dma(q, out, in_, outs=(), ins=()):
+        before(q, outs, ins, "dma")
+        sem = "d%d" % nd[0]
+        nd[0] += 1
+        tot[sem] = 16
+        eng[q].dma_start(out, in_).then_inc(T.sem[sem], 16)
+        after(q, outs, ins, sem, 16, "dma")
+
+    def lands(sem, val, regions):
+        tot[sem] = val
+        after("g", regions, (), sem, val, "remote")
+        snap[(sem, val)] = {}
+
+    def ts(out, i, s1, op0, s2=None, op1=None, off=None):
+        cols = [s for s in (s1, s2) if isinstance(s, tuple)]
+        a1 = ap(s1) if isinstance(s1, tuple) else s1
+        a2 = ap(s2) if isinstance(s2, tuple) else s2
+        src = ap(i) if off is None else ap(i).indirect(ap(off))
+        kw = {} if op1 is None else {"op1": op1}
+        op("v", [out], [i] + cols + ([off] if off else []),
+           lambda e: e.tensor_scalar(out=ap(out), in0=src, scalar1=a1, scalar2=a2, op0=op0, **kw))
+
+    def tt(out, a, b, o, off=None):
+        src = ap(a) if off is None else ap(a).indirect(ap(off))
+        op("v", [out], [a, b] + ([off] if off else []), lambda e: e.tensor_tensor(out=ap(out), in0=src, in1=ap(b), op=o))
+
+    def cp(out, i, off=None, scatter=None):
+        src = ap(i) if off is None else ap(i).indirect(ap(off))
+        dst = ap(out) if scatter is None else ap(out).indirect(ap(scatter))
+        op("v", [out], [i] + [o for o in (off, scatter) if o], lambda e: e.tensor_copy(out=dst, in_=src))
+
+    def scan(out, a, b, o0, o1):
+        op("v", [out], [a, b], lambda e: e.tensor_tensor_scan(out=ap(out), data0=ap(a), data1=ap(b), initial=0.0, op0=o0, op1=o1))
+
+    def red(out, i, o):
+        op("v", [out], [i], lambda e: e.tensor_reduce(out=ap(out), in_=ap(i), axis=AxisListType.X, op=o))
+
+    def fill(out, c):
+        op("v", [out], [], lambda e: e.memset(ap(out), c))
+
+    def act(out, i, fn, bias=None, scale=None, accum=None, off=None):
+        src = ap(i) if off is None else ap(i).indirect(ap(off))
+        kw = {}
+        if bias is not None:
+            kw["bias"] = ap(bias) if isinstance(bias, tuple) else bias
+        if scale is not None:
+            kw["scale"] = scale
+        if accum is not None:
+            kw["accum_out"] = ap(accum)
+        op("s", [out] + ([accum] if accum else []), [i] + [o for o in (bias, off) if isinstance(o, tuple)],
+           lambda e: e.activation(out=ap(out), in_=src, func=fn, **kw))
+
+    def quant(q, s, i):
+        op("v", [q, s], [i], lambda e: e.quantize_mx(ap(q), ap(s), ap(i)))
+
+    def mm(out, l, ls, r, rs, start=True, stop=True):
+        op("t", [out], [l, ls, r, rs], lambda e: e.matmul_mx(ap(out), ap(l), ap(ls), ap(r), ap(rs), start, stop), not start)
+
+    def iota(out, pattern, base, cm, flag=False):
+        kw = {"allow_small_or_imprecise_dtypes": True} if flag else {}
+        op("g", [out], [], lambda e: e.iota(ap(out), pattern, base, cm, **kw))
+
+    def select(out, i, pattern, cmp, c, base, cm):
+        op("g", [out], [i], lambda e: e.affine_select(ap(out), ap(i), pattern, cmp, c, base, cm))
+
+    def col(n):
+        return R(n, 0, 1)
+
+    def planes(x):
+        for b in range(4):
+            act(R("xp", 256 * b, 256 * b + 256), R(x, b, 1024, 4), F.Copy)
+
+    dma("y", ap(R("xi0")), T.x[:], [R("xi0")])
+    dma("s", ap(R("ub")), T.u[:], [R("ub")])
+    dma("y", ap(R("wq")).bitcast(dt.uint8), T.wc[:], [R("wq")])
+    dma("y", ap(R("wsc")), T.ws[:], [R("wsc")])
+    dma("y", ap(R("vb")), T.v[:], [R("vb")])
+    iota(R("iP"), [[0, 2]], 0, 1)
+    iota(R("iL"), [[16, 8]], 0, 0)
+    iota(R("fI"), [[1, 256]], 0, 0, True)
+    iota(R("iD"), [[0, 16], [1, 16]], 128, -1)
+    act(R("bigt"), R("fI"), F.Identity, bias=BIG, scale=0.0)
+    for b in (1, 2, 3):
+        act(R("cme", b, 1024, 4), R("fI"), F.Copy, scale=0.0)
+    iota(R("iC"), [[1, 8], [0, 64]], 0, 0)
+    select(R("d0"), R("bigt"), [[0, 16], [1, 16]], A.is_equal, -BIG, 0, 0)
+    iota(R("c16"), [[16, 16]], -1, 0, True)
+    iota(R("ek"), [[1, 2056]], 0, 0, True)
+    iota(R("iS"), [[0, 4], [16, 4]], 0, 1)
+    iota(R("k16"), [[16, 4], [0, 4]], 0, 0, True)
+    for c, k in enumerate((1, 3, 2, 0)):
+        iota(R("tb", 64 * c, 64 * c + 64), [[1, 64]], 64 * k, 0, True)
+    for a in range(4):
+        fill(R("cm%d" % a, 4 * 16 * (4 * a + 1), 4 * WD[a]), 0.0)
+    fill(R("rs", 0, 1), 0.0)
+    ts(R("pq"), R("iP"), 15, A.bitwise_and)
+    ts(R("pc"), R("pq"), 2, A.arith_shift_right)
+    cp(R("cf"), R("pc"))
+    ts(R("ch"), R("cf"), 2.0, A.is_ge)
+    ts(R("ca1"), R("cf"), 2.0, A.mult, 1.0, A.add)
+    ts(R("ca2"), R("cf"), 4.0, A.mult, -5.0, A.add)
+    tt(R("ca3"), R("ca2"), R("ch"), A.mult)
+    tt(R("kf"), R("ca1"), R("ca3"), A.subtract)
+    ts(R("ul", 0, 8), R("iL"), 4.0, A.add)
+    ts(R("ul", 8, 16), R("iL"), col("kf"), A.add)
+    ts(R("dl"), R("iD"), 15, A.bitwise_and)
+    ts(R("kk01"), R("dl"), 0.0, A.is_gt, 2.0 * BIG, A.mult)
+    act(R("maskb"), R("kk01"), F.Identity, bias=-BIG)
+    ts(R("pg"), R("iP"), 4, A.arith_shift_right)
+    cp(R("gpf"), R("pg"))
+    quant(R("qu"), R("su"), R("ub"))
+    op("v", [R("qu2")], [R("qu"), R("ul")],
+       lambda e: e.tensor_copy(ap(R("qu2")).bitcast(dt.uint32), ap(R("qu")).bitcast(dt.uint32).indirect(ap(R("ul")))))
+    act(R("su2"), R("su"), F.Copy, off=R("ul"))
+    act(R("io20"), R("fI"), F.Copy, scale=2.0 ** -20)
+    act(R("ones"), R("fI"), F.Identity, bias=1.0, scale=0.0)
+    quant(R("qx0"), R("sx0"), R("xi0"))
+    ts(R("gt"), R("iC"), col("gpf"), A.is_equal)
+    quant(R("qg"), R("sg"), R("gt"))
+
+    def late_constants():
+        ts(R("kc0"), R("kf"), -1.0, A.mult, 1027.0, A.add)
+        ts(R("pgf"), R("gpf"), 16.0, A.mult)
+        ts(R("s16p"), R("iS"), col("pgf"), A.subtract, -float(NO), A.add)
+        for b in range(4):
+            fill(R("xs", PT * b + 256, PT * b + PT), 0.0)
+        fill(R("hf"), 0.5)
+        select(R("ex"), R("hf"), [[-1, 516]], A.is_equal, 0.0, 3, 4)
+
+    def later_constants():
+        for b in range(4):
+            fill(R("dwn", PD * b + 256, PD * b + PD), 0.0)
+        fill(R("tb", 256, 264), -1.0)
+        quant(R("qv"), R("sv"), R("vb"))
+
+    rel = {(w, i): d for d, w, i in _relays(topo, T.cores, rank)}
+    nloc = [0]
+
+    def view(n, a, b, w):
+        v = T[n][:, a:b]
+        return v.bitcast(dt.uint8) if w == "c" else v
+
+    def send_two(ph, w, src, t):
+        before("g", (), [R(src)], "remote")
+        tr = []
+        for i in range(2):
+            rid, pid = topo.addr(rel[(w, i)], core)
+            en = topo.engines(core, rel[(w, i)])
+            h = len(en) // 2
+            en = en[i * h:i * h + h]
+            tr.append(RemoteDMATransfer(dst_ids=[DstId(rid=rid, pnc=pid)], dma_engine_mask=_mask(en), remote_sem=T.sem["r%s%s%d" % (w, ph, t)],
+                                        src=view(src, 64 * i, 64 * i + 64, w), dst=view("r%s%s%d" % (ph, w, t), 0, 64, w)))
+            nloc[0] += h
+        g.remote_dma_fused(tr, local_sem=T.sem.loc)
+
+    def send_one(ph, w, src, a, dst, to, land, t):
+        before("g", (), [R(src, a, a + 64)], "remote")
+        rid, pid = topo.addr(dst, core)
+        en = topo.engines(core, dst)
+        g.remote_dma(out_ap=view(land, to, to + 64, w), in_ap=view(src, a, a + 64, w), remote_sem=T.sem["ad%s%d" % (ph, t)],
+                     local_sem=T.sem.loc, pid=pid, routing_id=rid, dma_engine_mask=_mask(en))
+        nloc[0] += len(en)
+
+    def layer(qb, sb, off, z, qz, sz, h, qh, sh, hoff):
+        for b in range(4):
+            mm(R("pd", 512 * b, 512 * b + 128), R("qe%d" % b), R("se%d" % b), R(qb, off, off + 128), R(sb, off, off + 128))
+        for b in range(4):
+            tt(R(z, b, 512, 4), R("pd", 512 * b, 512 * b + 128), R("e2x", 128 * b, 128 * b + 128), A.add)
+        quant(R(qz), R(sz), R(z))
+        for b in (2, 0, 3, 1):
+            mm(R("pr", 512 * b, 512 * b + 128), R("wq", 128 * b, 128 * b + 128), R("wsc", 128 * b, 128 * b + 128), R(qz), R(sz))
+        for b in (2, 0, 3, 1):
+            o, i = R(h, b, 512, 4), R("pr", 512 * b, 512 * b + 128)
+            if b < 2:
+                ts(o, i, 0.03125, A.mult)
+            else:
+                act(o, i, F.Copy, scale=0.03125)
+        quant(R(qh, hoff, hoff + 128), R(sh, hoff, hoff + 128), R(h))
+
+    def unpack(q, s, off, to):
+        for b in (2, 0, 3, 1):
+            mm(R("pd", 512 * b, 512 * b + 128), R("qe%d" % b), R("se%d" % b), R(q, off, off + 128), R(s, off, off + 128))
+        for b in (2, 0, 3, 1):
+            o, i = R("dwn", PD * b + to, PD * b + to + 128), R("pd", 512 * b, 512 * b + 128)
+            if b < 2:
+                ts(o, i, 2.0, A.mult)
+            else:
+                act(o, i, F.Copy, scale=2.0)
+
+    def count(n, m, bias):
+        act(R("junk2", 256 * n - 256, 256 * n), R("cum"), F.Sign, bias=bias, scale=-float(m), accum=col("ac%d" % n))
+
+    def answer(n, kc):
+        ts(col("ky%d" % n), col("ac%d" % n), -4.0, A.mult, col(kc), A.add)
+        cp(R("ck%d" % n), R("ek"), off=col("ky%d" % n))
+        red(col("km%d" % n), R("ck%d" % n), A.max)
+
+    def edge(n):
+        act(col("fr%d" % n), col("km%d" % n), F.Identity, bias=257.375, scale=-0.125)
+        act(col("e%d" % n), col("km%d" % n), F.Identity, bias=256.875 - NO, scale=-0.125)
+
+    def place(n):
+        ts(col("ao%d" % n), col("km%d" % n), -0.125, A.mult, 256.375, A.add)
+
+    for t in range(2):
+        X, Q, S = "xi%d" % t, "qx%d" % t, "sx%d" % t
+        pa, pv, pc = R("pr", 0, 256), R("pr", 512, 768), R("pr", 1024, 1280)
+        mm(pa, R("qu2", 0, 128), R("su2", 0, 128), R(Q), R(S))
+        mm(pv, R("qu2", 128, 256), R("su2", 128, 256), R(Q), R(S))
+        mm(R("pr", 1536, 1792), R("qu2", 0, 128), R("su2", 0, 128), R(Q), R(S))
+        act(R("sg1"), pv, F.Sign)
+        act(R("sg2"), R("sg1"), F.Relu)
+        tt(R("dd"), pa, R("maskb"), A.max)
+        scan(R("ow"), R("d0"), R("dd"), A.max, A.min)
+        share = (15, 14) if t == 0 else (15, 14, 13)
+        for m in share:
+            own, e, n = R("ow", 16 * m + 15, 16 * m + 16), m - 12, 16 * m
+            act(R("rl%d" % m, 0, n + 16), R("pr", 1536, 1552 + n), F.Relu, bias=own, scale=-1.0)
+            act(R("cm3", e, 4 * n, 4), R("rl%d" % m, 0, n), F.Sign, accum=R("rs", m, m + 1))
+            act(R("cm3", 4 * n + e, 4 * n + 64, 4), R("rl%d" % m, n, n + 16), F.Sign)
+        tt(R("cme", 0, 1024, 4), pa, R("ow"), A.is_equal)
+        quant(R("qce"), R("sce"), R("cme"))
+        mm(pc, R("qg"), R("sg"), R("qce"), R("sce"), True, False)
+        for m in (13, 12, 11, 10, 9, 8, "q2", 7, 6, 5, 4, "q1", "q3", 3, 2, 1, 0, "q0"):
+            if m in share:
+                continue
+            if isinstance(m, int):
+                a, e = m // 4, m % 4
+                ts(R("cm%d" % a, e, 64 * m + 64, 4), R("pr", 0, 16 * m + 16), R("ow", 16 * m + 15, 16 * m + 16), A.is_lt)
+                if m:
+                    act(R("junk", 8 * m * (m - 1), 8 * m * (m + 1)), R("cm%d" % a, e, 64 * m, 4), F.Copy, accum=R("rs", m, m + 1))
+            else:
+                a = int(m[1])
+                quant(R("qc%d" % a), R("sc%d" % a), R("cm%d" % a))
+                mm(R("pr", 1024, 1024 + WD[a]), R("qg"), R("sg"), R("qc%d" % a), R("sc%d" % a), False, a == 0)
+        planes(X)
+        tt(R("pay"), R("sg2"), R("io20"), A.add)
+        tt(R("rt"), R("rs"), R("c16"), A.subtract)
+        tt(R("dw2"), pc, R("maskb"), A.max)
+        scan(R("ow2"), R("d0"), R("dw2"), A.max, A.min)
+        tt(R("rk"), R("ow2", 15, 256, 16), R("rt"), A.subtract)
+        cp(R("ro"), R("rk"))
+        cp(R("win"), R("pay"), scatter=R("ro"))
+        scan(R("cum"), R("win"), R("ones"), A.add, A.add)
+        ts(col("tm"), R("cum", 255, 256), -0.5, A.add)
+        count(1, 4, col("tm"))
+        if t == 0:
+            late_constants()
+        tt(R("dw3"), R("win"), R("maskb"), A.max)
+        answer(1, "kc0")
+        edge(1)
+        place(1)
+        ts(R("bs2"), R("cum"), 2.0, A.mult, col("tm"), A.add, off=col("ao1"))
+        count(2, 3, R("bs2", 0, 1))
+        ts(col("kx1"), col("ky1"), col("km1"), A.is_equal, -5000.0, A.mult)
+        tt(col("kcb"), col("kx1"), col("kc0"), A.add)
+        scan(R("ow3"), R("d0"), R("dw3"), A.max, A.min)
+        answer(2, "kcb")
+        edge(2)
+        place(2)
+        ts(R("bs3"), R("cum"), 1.0, A.mult, col("tm"), A.add, off=col("ao2"))
+        count(3, 2, R("bs3", 0, 1))
+        ts(R("bt"), R("ow3", 15, 256, 16), 1.0, A.is_ge)
+        ts(col("kx2"), col("ky2"), col("km2"), A.is_equal, -5000.0, A.mult)
+        tt(R("io"), R("ow3", 15, 256, 16), R("bt"), A.subtract)
+        tt(col("kcc"), col("kx2"), col("kcb"), A.add)
+        ts(R("ol"), R("io"), 2.0 ** 20, A.mult)
+        for b in range(4):
+            act(R("xs", PT * b, PT * b + 256), R("xp", 256 * b, 256 * b + 256), F.Copy, off=R("ol"))
+        ts(R("t1"), R("ck2"), col("km2"), A.is_equal, col("fr1"), A.mult)
+        ts(R("xa"), R("ck1"), col("km1"), A.is_equal, col("e1"), A.mult)
+        ts(R("xb"), R("ck2"), col("km2"), A.is_equal, col("e2"), A.mult)
+        tt(R("t1"), R("t1"), R("s16p"), A.add)
+        tt(R("xa"), R("xa"), R("xb"), A.add)
+        answer(3, "kcc")
+        ts(col("fr3"), col("km3"), -0.125, A.mult, 257.375, A.add)
+        ts(col("em"), col("km3"), -0.125, A.mult, 256.875 - NO, A.add)
+        ts(col("dda"), col("fr3"), -1.0, A.mult, col("fr2"), A.add)
+        ts(R("t3"), R("ck3"), 0.0, A.is_gt, col("fr3"), A.mult)
+        ts(R("en"), R("ck3"), col("km3"), A.is_equal, col("em"), A.mult)
+        ts(R("t2"), R("ck3"), col("km3"), A.is_equal, col("dda"), A.mult)
+        tt(R("t1"), R("t1"), R("t3"), A.add)
+        tt(R("en"), R("en"), R("xa"), A.add)
+        tt(R("t1"), R("t1"), R("t2"), A.add)
+        tt(R("vl"), R("t1"), R("en"), A.is_lt)
+        tt(R("plf"), R("t1"), R("vl"), A.mult)
+        ts(R("pl"), R("plf"), float(NO), A.add)
+        for o, lo, q, s in (("b13", 0, "qb%d" % t, "sb%d" % t), ("b02", 8, "wbc%d" % t, "wbs%d" % t)):
+            for b in (2, 0, 3, 1):
+                if b < 2:
+                    cp(R(o, b, 512, 4), R("xs", PT * b, PT * b + PT), off=R("pl", lo, lo + 8))
+                else:
+                    act(R(o, b, 512, 4), R("xs", PT * b, PT * b + PT), F.Copy, off=R("pl", lo, lo + 8))
+            quant(R(q, 0, 128), R(s, 0, 128), R(o))
+            if lo == 0:
+                send_two("b", "c", q, t)
+                send_two("b", "s", s, t)
+        d2 = T.cores[(rank + 2) % N]
+        send_one("b", "c", "wbc%d" % t, 0, d2, 128, "wbc%d" % t, t)
+        send_one("b", "s", "wbs%d" % t, 0, d2, 128, "wbs%d" % t, t)
+        for b in range(4):
+            for k in range(2):
+                act(R("e2x", 128 * b + 64 * k, 128 * b + 64 * k + 64), R("xs", PT * b, PT * b + 64), F.Copy, scale=0.5)
+        if t == 0:
+            for b in range(4):
+                quant(R("qe%d" % b), R("se%d" % b), R("ex", 3 - b, 515 - b))
+        lands("adb%d" % t, 16, [R("wbc%d" % t, 128, 192), R("wbs%d" % t, 128, 192)])
+        lands("aob%d" % t, 32, [R("lbc%d" % t), R("lbs%d" % t)])
+        layer("wbc%d" % t, "wbs%d" % t, 64, "za", "qza", "sza", "ha", "whc%d" % t, "whs%d" % t, 64)
+        p2 = T.cores[(rank - 2) % N]
+        send_one("h", "c", "whc%d" % t, 128, p2, 0, "whc%d" % t, t)
+        send_one("h", "s", "whs%d" % t, 128, p2, 0, "whs%d" % t, t)
+        layer("lbc%d" % t, "lbs%d" % t, 0, "zb", "qzb", "szb", "hb", "qh%d" % t, "sh%d" % t, 0)
+        send_two("h", "c", "qh%d" % t, t)
+        send_two("h", "s", "sh%d" % t, t)
+        if t == 0:
+            later_constants()
+        place(3)
+        for n in (1, 2, 3):
+            ts(col("af%d" % n), col("ao%d" % n), 1.0, A.add)
+            ts(R("w%d" % n), R("ck%d" % n), col("km%d" % n), A.is_equal)
+            tt(R("c%d" % n), R("w%d" % n), R("k16"), A.mult)
+            red(col("cb%d" % n), R("c%d" % n), A.add)
+        tt(col("cb4"), col("cb1"), col("cb2"), A.add)
+        tt(col("cb4"), col("cb4"), col("cb3"), A.add)
+        ts(col("cb4"), col("cb4"), -1.0, A.mult, 384.0, A.add)
+        for n in (2, 3, 4):
+            tt(col("db%d" % n), col("cb%d" % n), col("cb%d" % (n - 1)), A.subtract)
+        tt(col("da2"), col("af2"), col("af1"), A.subtract)
+        tt(col("da3"), col("af3"), col("af2"), A.subtract)
+        for n, d in ((1, "af1"), (2, "da2"), (3, "da3")):
+            ts(R("y%d" % n), R("rk"), col("af%d" % n), A.is_ge, col(d), A.mult)
+            ts(R("z%d" % n), R("rk"), col("af%d" % n), A.is_ge, col("db%d" % (n + 1)), A.mult)
+        tt(R("rl"), R("rk"), R("y1"), A.subtract)
+        tt(R("rl"), R("rl"), R("y2"), A.subtract)
+        tt(R("rl"), R("rl"), R("y3"), A.subtract)
+        ts(R("sv1"), R("rl"), col("cb1"), A.add, -256.0, A.add)
+        for n in (1, 2, 3):
+            tt(R("sv1"), R("sv1"), R("z%d" % n), A.add)
+        ts(R("vl"), R("rl"), 64.0, A.is_lt)
+        tt(R("sf"), R("sv1"), R("vl"), A.mult)
+        ts(R("so"), R("sf"), 256.0, A.add)
+        if t == 1:
+            act(R("slr"), R("tb"), F.Copy, off=R("so"))
+            dma("y", T.sl[:], T.slr[0:128:16, :], (), [R("slr")])
+        lands("adh%d" % t, 16, [R("whc%d" % t, 0, 64), R("whs%d" % t, 0, 64)])
+        lands("aoh%d" % t, 32, [R("lhc%d" % t), R("lhs%d" % t)])
+        unpack("whc%d" % t, "whs%d" % t, 0, 128)
+        unpack("lhc%d" % t, "lhs%d" % t, 0, 0)
+        X2 = "xi%d" % (t + 1)
+        for b in range(4):
+            tt(R(X2, b, 1024, 4), R("dwn", PD * b, PD * b + PD), R(X, b, 1024, 4), A.add, off=R("so"))
+        quant(R("qx%d" % (t + 1)), R("sx%d" % (t + 1)), R(X2))
+    mm(R("pr", 0, 256), R("qv"), R("sv"), R("qx2"), R("sx2"))
+    dma("y", T.oc[:], ap(R("qx2")).bitcast(dt.uint8), (), [R("qx2")])
+    for k in range(4):
+        dma("s" if k % 2 else "y", T.osc[4 * k:4 * k + 4, :], T.sx2[32 * k:32 * k + 4, :], (), [R("sx2")])
+    act(R("ycp"), R("pr", 0, 256), F.Copy)
+    dma("s", T.y[:], ap(R("ycp")), (), [R("ycp")])
+    tot["loc"] = nloc[0]
+    for sem in sorted(tot):
+        wait("g", sem, tot[sem])

@@ -2,14 +2,28 @@ from concourse.bass import DstId, RemoteDMATransfer
 from concourse.mybir import dt, AluOpType as A, AxisListType, ActivationFunctionType as F
 
 N = 8
-BIG = float(2.0 ** 90)
-PT = 336
-NO = 320
-PD = 272
-WD = (128, 128, 192, 256)
+C = 256
+PT = 320
+WD = (256, 256, 128, 128)
+LANE = {15: (0, 1), 14: (0, 2), 13: (0, 3)}
+LANE.update({m: (1 + (12 - m) // 4, (12 - m) % 4) for m in range(1, 13)})
+EPS = 2.0 ** -22
+U9 = 2.0 ** -9
 SCRATCH = {}
 PLACE = {}
 PSUM = ("pr", "pd")
+
+
+def _spans():
+    lo, hi, out = 0, 0, []
+    for m in (4, 3, 2):
+        lo, hi = lo - (-(C - lo) // (2 * m - 1)), hi - (-2 * (C - hi) // (m + 1))
+        out.append((lo, hi))
+    return out
+
+
+SPAN = _spans()
+E3, EK = 2 * SPAN[2][0], 2 * SPAN[2][1] + 2
 
 
 def _decl():
@@ -32,21 +46,21 @@ def _decl():
     add("qu qv", 128, q), add("su sv", 128, s)
     add("qu2", 256, q), add("su2", 256, s)
     add("wq", 512, q), add("wsc", 512, s)
-    share("ci", i, ("iD dl", 256), ("iC", 512), ("iL", 8), ("iP pq pc pg", 2), ("iS", 16))
-    share("cfl", f, ("fI maskb d0 ones io20 kk01 bigt", 256), ("ek", 2056), ("tb", 264), ("cf ch ca1 ca2 ca3 kf kc0 pgf gpf", 2), ("s16p c16 k16", 16))
+    share("ci", i, ("iP pq pb2 pb3 pg", 2))
+    share("cfl", f, ("jm ab mk d0 z16 dx mx kc c15", 256), ("ek", EK), ("ek3 ek3n", EK - E3 + 8), ("tb", 512),
+          ("pf k1 kf kfo gpf p4 p4m cro pfm", 2), ("iL", 8), ("c16 kq kfr kfr9 s1 s2 cj", 16), ("fr4", 4), ("d4 z4", 64))
     add("ul", 16, h)
-    add("gt", 512, b), add("hf ex", 516, b)
-    share("qk", q, ("qg qe0 qe1 qe2 qe3", 128)), share("sk", s, ("sg se0 se1 se2 se3", 128))
+    add("gt iC", 512, b), add("hf ex eh", 516, b), add("dv", 256, b)
+    share("qk", q, ("qg qe0 qe1 qe2 qe3 qf0 qf1 qf2 qf3", 128)), share("sk", s, ("sg se0 se1 se2 se3 sf0 sf1 sf2 sf3", 128))
     for k in range(4):
         add("cm%d" % k, 4 * WD[k], b)
-    add("cme", 1024, b)
-    share("qc", q, ("qc0 qc1", 128), ("qc2", 192), ("qc3 qce", 256)), share("sc", s, ("sc0 sc1", 128), ("sc2", 192), ("sc3 sce", 256))
-    add("dd ow sg1 sg2 pay dw2 ow2 win cum dw3 ow3 ycp slr", 256, f), add("junk", 1920, b), add("junk2", 768, b)
-    add("rl13 rl14 rl15", 256, b)
-    share("sm", f, ("rs rt rk ck1 ck2 ck3 bs2 bs3 bt io w1 w2 w3 xa xb t1 t2 t3 en vl plf c1 c2 c3 z1 z2 z3 y1 y2 y3 sv1 rl sf", 16),
-          ("tm ac1 ac2 ac3 km1 km2 km3 kx1 kx2 kcb kcc fr1 fr2 fr3 dda em af1 af2 af3 cb1 cb2 cb3 cb4 db2 db3 db4 da2 da3 e1 e2", 2))
-    share("li", h, ("ro pl so ol", 16), ("ky1 ky2 ky3 ao1 ao2 ao3", 2))
-    add("xp", 1024, b), add("xs", 4 * PT, b), add("e2x", 512, b), add("dwn", 4 * PD, b)
+    share("qc", q, *[("qc%d" % k, WD[k]) for k in range(4)]), share("sc", s, *[("sc%d" % k, WD[k]) for k in range(4)])
+    add("dd ow sgn pay exr win exw ycp slr", 256, f), add("cum", 520, f), add("v1", 256, b)
+    add("junk", 1920, b), add("junk2", 384, b), add("rl13 rl14 rl15", 256, b)
+    share("sm", f, ("rs rt rk sq g1 g2 key1 key2 key3 kn3 m1 m2 m3 f2 r1 w sa sb st", 16), ("ii ff gg hh", 32), ("qq qo uu uo", 64),
+          ("ac1 ac2 ac3 bs1 bs2 km1 km2 km3 ex1 ex2", 2), ("ft ft2", 4))
+    share("li", h, ("ro pl so ol ri", 16), ("id1 id2 id3", 2))
+    add("xp", 2048, b), add("xs", 4 * PT, b), add("e2x", 512, b)
     add("b13 b02 za zb ha hb", 512, b), add("qza qzb", 128, q), add("sza szb", 128, s)
     for t in range(3):
         add("xi%d" % t, 1024, b), add("qx%d" % t, 256, q), add("sx%d" % t, 256, s)
@@ -187,8 +201,8 @@ def rank_program(g, core, T, topo):
         dst = ap(out) if scatter is None else ap(out).indirect(ap(scatter))
         op("v", [out], [i] + [o for o in (off, scatter) if o], lambda e: e.tensor_copy(out=dst, in_=src))
 
-    def scan(out, a, b, o0, o1):
-        op("v", [out], [a, b], lambda e: e.tensor_tensor_scan(out=ap(out), data0=ap(a), data1=ap(b), initial=0.0, op0=o0, op1=o1))
+    def scan(out, a, b, o0, o1, first=0.0):
+        op("v", [out], [a, b], lambda e: e.tensor_tensor_scan(out=ap(out), data0=ap(a), data1=ap(b), initial=first, op0=o0, op1=o1))
 
     def red(out, i, o):
         op("v", [out], [i], lambda e: e.tensor_reduce(out=ap(out), in_=ap(i), axis=AxisListType.X, op=o))
@@ -208,13 +222,19 @@ def rank_program(g, core, T, topo):
         op("s", [out] + ([accum] if accum else []), [i] + [o for o in (bias, off) if isinstance(o, tuple)],
            lambda e: e.activation(out=ap(out), in_=src, func=fn, **kw))
 
+    def pick(q, out, i, off):
+        if q == "v":
+            cp(out, i, off=off)
+        else:
+            act(out, i, F.Copy, off=off)
+
     def quant(q, s, i):
         op("v", [q, s], [i], lambda e: e.quantize_mx(ap(q), ap(s), ap(i)))
 
     def mm(out, l, ls, r, rs, start=True, stop=True):
         op("t", [out], [l, ls, r, rs], lambda e: e.matmul_mx(ap(out), ap(l), ap(ls), ap(r), ap(rs), start, stop), not start)
 
-    def iota(out, pattern, base, cm, flag=False):
+    def iota(out, pattern, base, cm, flag=True):
         kw = {"allow_small_or_imprecise_dtypes": True} if flag else {}
         op("g", [out], [], lambda e: e.iota(ap(out), pattern, base, cm, **kw))
 
@@ -224,71 +244,90 @@ def rank_program(g, core, T, topo):
     def col(n):
         return R(n, 0, 1)
 
-    def planes(x):
-        for b in range(4):
-            act(R("xp", 256 * b, 256 * b + 256), R(x, b, 1024, 4), F.Copy)
+    def plane(x, b):
+        act(R("xp", 512 * b, 512 * b + 256), R(x, b, 1024, 4), F.Copy)
 
     dma("y", ap(R("xi0")), T.x[:], [R("xi0")])
     dma("s", ap(R("ub")), T.u[:], [R("ub")])
-    dma("y", ap(R("wq")).bitcast(dt.uint8), T.wc[:], [R("wq")])
-    dma("y", ap(R("wsc")), T.ws[:], [R("wsc")])
-    dma("y", ap(R("vb")), T.v[:], [R("vb")])
-    iota(R("iP"), [[0, 2]], 0, 1)
+    iota(R("iP"), [[0, 2]], 0, 1, False)
+    iota(R("jm"), [[0, 16], [-4096, 16]], 0, 0)
     iota(R("iL"), [[16, 8]], 0, 0)
-    iota(R("fI"), [[1, 256]], 0, 0, True)
-    iota(R("iD"), [[0, 16], [1, 16]], 128, -1)
-    act(R("bigt"), R("fI"), F.Identity, bias=BIG, scale=0.0)
-    for b in (1, 2, 3):
-        act(R("cme", b, 1024, 4), R("fI"), F.Copy, scale=0.0)
+    iota(R("kq"), [[-1, 2], [2, 2], [0, 4]], 1, 0)
+    iota(R("s1"), [[0, 4], [32, 4]], 0, 0)
     iota(R("iC"), [[1, 8], [0, 64]], 0, 0)
-    select(R("d0"), R("bigt"), [[0, 16], [1, 16]], A.is_equal, -BIG, 0, 0)
-    iota(R("c16"), [[16, 16]], -1, 0, True)
-    iota(R("ek"), [[1, 2056]], 0, 0, True)
-    iota(R("iS"), [[0, 4], [16, 4]], 0, 1)
-    iota(R("k16"), [[16, 4], [0, 4]], 0, 0, True)
-    for c, k in enumerate((1, 3, 2, 0)):
-        iota(R("tb", 64 * c, 64 * c + 64), [[1, 64]], 64 * k, 0, True)
-    for a in range(4):
-        fill(R("cm%d" % a, 4 * 16 * (4 * a + 1), 4 * WD[a]), 0.0)
-    fill(R("rs", 0, 1), 0.0)
+    iota(R("c16"), [[16, 16]], 15, 0)
+    iota(R("rs", 0, 1), [[0, 1]], 0, 0)
+    iota(R("ek"), [[1, EK]], 0, 0)
+    iota(R("cum"), [[0, 520]], 4096, 0)
+    iota(R("d4"), [[0, 16], [-64, 4]], 64, 0)
+    for b in range(4):
+        iota(R("xs", PT * b + 256, PT * b + PT), [[0, PT - 256]], 0, 0)
+
+    def more_iotas():
+        iota(R("ek", 0, 8), [[0, 8]], 4096, 0)
+        iota(R("ek3", 0, 8), [[0, 8]], 64, 0)
+        iota(R("ek3n", 0, 8), [[0, 8]], -1, 0)
+        iota(R("hf"), [[0, 516]], 1, 0)
+        select(R("ex"), R("hf"), [[-1, 516]], A.is_equal, 0.0, 3, 4)
+        iota(R("fr4"), [[1, 4]], 0, 0)
+        iota(R("z4"), [[0, 16], [4096, 4]], 0, 0)
+        iota(R("tb", 0, 256), [[0, 256]], -1, 0)
+        iota(R("tb", 256, 384), [[128, 2], [1, 64]], 64, 0)
+        iota(R("tb", 384, 512), [[128, 2], [1, 64]], 0, 0)
+    for a, lo in enumerate((208, 144, 80, 16)):
+        fill(R("cm%d" % a, 4 * lo, 4 * WD[a]), 0.0)
+    fill(R("dv"), -64.0)
     ts(R("pq"), R("iP"), 15, A.bitwise_and)
-    ts(R("pc"), R("pq"), 2, A.arith_shift_right)
-    cp(R("cf"), R("pc"))
-    ts(R("ch"), R("cf"), 2.0, A.is_ge)
-    ts(R("ca1"), R("cf"), 2.0, A.mult, 1.0, A.add)
-    ts(R("ca2"), R("cf"), 4.0, A.mult, -5.0, A.add)
-    tt(R("ca3"), R("ca2"), R("ch"), A.mult)
-    tt(R("kf"), R("ca1"), R("ca3"), A.subtract)
+    ts(R("pb2"), R("iP"), 2, A.arith_shift_right, 1, A.bitwise_and)
+    ts(R("pb3"), R("iP"), 3, A.arith_shift_right, 1, A.bitwise_and)
+    ts(R("p4"), R("pq"), 4096.0, A.mult)
+    ts(R("k1"), R("pb2"), 2.0, A.mult, 1.0, A.add)
+    ts(R("pg"), R("iP"), 4, A.arith_shift_right)
+    tt(R("kf"), R("k1"), R("pb3"), A.subtract)
+    ts(R("p4m"), R("pq"), 4096.0, A.mult, -300.0, A.add)
+    cp(R("gpf"), R("pg"))
+    ts(R("pf"), R("pq"), -1.0, A.mult)
+    ts(R("cro"), R("pq"), 300.0, A.mult, 3392.0, A.add)
     ts(R("ul", 0, 8), R("iL"), 4.0, A.add)
     ts(R("ul", 8, 16), R("iL"), col("kf"), A.add)
-    ts(R("dl"), R("iD"), 15, A.bitwise_and)
-    ts(R("kk01"), R("dl"), 0.0, A.is_gt, 2.0 * BIG, A.mult)
-    act(R("maskb"), R("kk01"), F.Identity, bias=-BIG)
-    ts(R("pg"), R("iP"), 4, A.arith_shift_right)
-    cp(R("gpf"), R("pg"))
+    act(R("ab"), R("jm"), F.Abs, bias=col("p4"))
+    act(R("d0"), R("jm"), F.Identity, bias=-2.0 ** 91, scale=-2.0 ** 80)
+    act(R("mk"), R("ab"), F.Identity, bias=2.0 ** 91, scale=-2.0 ** 80)
+    ts(R("pfm"), R("pq"), 2.0, A.mult, 0.5, A.add)
     quant(R("qu"), R("su"), R("ub"))
     op("v", [R("qu2")], [R("qu"), R("ul")],
        lambda e: e.tensor_copy(ap(R("qu2")).bitcast(dt.uint32), ap(R("qu")).bitcast(dt.uint32).indirect(ap(R("ul")))))
     act(R("su2"), R("su"), F.Copy, off=R("ul"))
-    act(R("io20"), R("fI"), F.Copy, scale=2.0 ** -20)
-    act(R("ones"), R("fI"), F.Identity, bias=1.0, scale=0.0)
     quant(R("qx0"), R("sx0"), R("xi0"))
+    act(R("z16"), R("jm"), F.Sign, scale=-1.0)
+    before("y", (), [R("xi0")], "dma")
+    dma("y", ap(R("wq")).bitcast(dt.uint8), T.wc[:], [R("wq")])
+    dma("y", ap(R("wsc")), T.ws[:], [R("wsc")])
+    dma("y", ap(R("vb")), T.v[:], [R("vb")])
     ts(R("gt"), R("iC"), col("gpf"), A.is_equal)
-    quant(R("qg"), R("sg"), R("gt"))
+
+    def tail_constants():
+        act(R("c15"), R("jm"), F.Identity, bias=1.5, scale=0.0)
+        act(R("mx", 15, 256, 16), R("mx", 15, 256, 16), F.Copy, scale=2.0 ** -121)
+        act(R("kfr"), R("kq"), F.Copy, scale=0.0625)
+        act(R("kfo"), R("kf"), F.Copy, scale=0.0625)
+        act(R("s2"), R("s1"), F.Identity, bias=col("pfm"))
+        act(R("kfr9"), R("kq"), F.Copy, scale=0.0625 * U9)
+        act(R("ff", 0, 32, 2), R("s2"), F.Copy, scale=U9)
+        act(R("gg", 0, 32, 2), R("s2"), F.Copy, scale=U9)
+        act(R("ek3", 8), R("ek", E3, EK), F.Copy, scale=U9)
+        act(R("ek3n", 8), R("ek", E3, EK), F.Copy, scale=U9)
 
     def late_constants():
-        ts(R("kc0"), R("kf"), -1.0, A.mult, 1027.0, A.add)
-        ts(R("pgf"), R("gpf"), 16.0, A.mult)
-        ts(R("s16p"), R("iS"), col("pgf"), A.subtract, -float(NO), A.add)
         for b in range(4):
-            fill(R("xs", PT * b + 256, PT * b + PT), 0.0)
-        fill(R("hf"), 0.5)
-        select(R("ex"), R("hf"), [[-1, 516]], A.is_equal, 0.0, 3, 4)
+            quant(R("qe%d" % b), R("se%d" % b), R("eh", 3 - b, 515 - b))
 
     def later_constants():
         for b in range(4):
-            fill(R("dwn", PD * b + 256, PD * b + PD), 0.0)
-        fill(R("tb", 256, 264), -1.0)
+            quant(R("qf%d" % b), R("sf%d" % b), R("ex", 3 - b, 515 - b))
+        ts(R("pfm"), R("pq"), -1.0, A.add)
+        ts(R("fr4"), R("fr4"), 0.125, A.mult)
+        ts(R("cj"), R("c16"), col("pf"), A.subtract, -15.0, A.add)
         quant(R("qv"), R("sv"), R("vb"))
 
     rel = {(w, i): d for d, w, i in _relays(topo, T.cores, rank)}
@@ -311,54 +350,53 @@ def rank_program(g, core, T, topo):
             nloc[0] += h
         g.remote_dma_fused(tr, local_sem=T.sem.loc)
 
-    def send_one(ph, w, src, a, dst, to, land, t):
+    def send_one(ph, w, src, a, dst, to, t):
         before("g", (), [R(src, a, a + 64)], "remote")
         rid, pid = topo.addr(dst, core)
         en = topo.engines(core, dst)
-        g.remote_dma(out_ap=view(land, to, to + 64, w), in_ap=view(src, a, a + 64, w), remote_sem=T.sem["ad%s%d" % (ph, t)],
+        g.remote_dma(out_ap=view(src, to, to + 64, w), in_ap=view(src, a, a + 64, w), remote_sem=T.sem["ad%s%d" % (ph, t)],
                      local_sem=T.sem.loc, pid=pid, routing_id=rid, dma_engine_mask=_mask(en))
         nloc[0] += len(en)
 
-    def layer(qb, sb, off, z, qz, sz, h, qh, sh, hoff):
+    def bank(ps, b):
+        return R(ps, 512 * b, 512 * b + 128)
+
+    def unpack(ps, e, q, s, off):
         for b in range(4):
-            mm(R("pd", 512 * b, 512 * b + 128), R("qe%d" % b), R("se%d" % b), R(qb, off, off + 128), R(sb, off, off + 128))
+            mm(bank(ps, b), R("q%s%d" % (e, b)), R("s%s%d" % (e, b)), R(q, off, off + 128), R(s, off, off + 128))
+
+    def mix(ps, z):
         for b in range(4):
-            tt(R(z, b, 512, 4), R("pd", 512 * b, 512 * b + 128), R("e2x", 128 * b, 128 * b + 128), A.add)
-        quant(R(qz), R(sz), R(z))
+            tt(R(z, b, 512, 4), bank(ps, b), R("e2x", 128 * b, 128 * b + 128), A.add)
+        quant(R("q" + z), R("s" + z), R(z))
+
+    def layer(ps, z):
         for b in (2, 0, 3, 1):
-            mm(R("pr", 512 * b, 512 * b + 128), R("wq", 128 * b, 128 * b + 128), R("wsc", 128 * b, 128 * b + 128), R(qz), R(sz))
+            mm(bank(ps, b), R("wq", 128 * b, 128 * b + 128), R("wsc", 128 * b, 128 * b + 128), R("q" + z), R("s" + z))
+
+    def scaled(ps, h, qh, sh):
         for b in (2, 0, 3, 1):
-            o, i = R(h, b, 512, 4), R("pr", 512 * b, 512 * b + 128)
             if b < 2:
-                ts(o, i, 0.03125, A.mult)
+                ts(R(h, b, 512, 4), bank(ps, b), 0.03125, A.mult)
             else:
-                act(o, i, F.Copy, scale=0.03125)
-        quant(R(qh, hoff, hoff + 128), R(sh, hoff, hoff + 128), R(h))
+                act(R(h, b, 512, 4), bank(ps, b), F.Copy, scale=0.03125)
+        quant(R(qh, 0, 128), R(sh, 0, 128), R(h))
 
-    def unpack(q, s, off, to):
-        for b in (2, 0, 3, 1):
-            mm(R("pd", 512 * b, 512 * b + 128), R("qe%d" % b), R("se%d" % b), R(q, off, off + 128), R(s, off, off + 128))
-        for b in (2, 0, 3, 1):
-            o, i = R("dwn", PD * b + to, PD * b + to + 128), R("pd", 512 * b, 512 * b + 128)
-            if b < 2:
-                ts(o, i, 2.0, A.mult)
-            else:
-                act(o, i, F.Copy, scale=2.0)
+    def renew(ps, old, to):
+        for b in range(4):
+            tt(R("xp", 512 * b + to, 512 * b + to + 128), bank(ps, b), R(old, b, 512, 4), A.add)
 
-    def count(n, m, bias):
-        act(R("junk2", 256 * n - 256, 256 * n), R("cum"), F.Sign, bias=bias, scale=-float(m), accum=col("ac%d" % n))
+    def count(n, bias):
+        lo, hi = SPAN[n - 1]
+        act(R("junk2", 128 * n - 128, 128 * n - 128 + hi - lo), R("cum", 2 * lo, 2 * hi, 2), F.Sign, bias=bias, scale=float(n - 5),
+            accum=col("ac%d" % n))
 
-    def answer(n, kc):
-        ts(col("ky%d" % n), col("ac%d" % n), -4.0, A.mult, col(kc), A.add)
-        cp(R("ck%d" % n), R("ek"), off=col("ky%d" % n))
-        red(col("km%d" % n), R("ck%d" % n), A.max)
-
-    def edge(n):
-        act(col("fr%d" % n), col("km%d" % n), F.Identity, bias=257.375, scale=-0.125)
-        act(col("e%d" % n), col("km%d" % n), F.Identity, bias=256.875 - NO, scale=-0.125)
-
-    def place(n):
-        ts(col("ao%d" % n), col("km%d" % n), -0.125, A.mult, 256.375, A.add)
+    def answer(n):
+        lo, hi = SPAN[n - 1]
+        if n == 1:
+            ts(col("id1"), col("ac1"), float(lo + hi), A.add)
+        else:
+            ts(col("id%d" % n), col("ac%d" % n), float(lo + hi - (E3 - 8 if n == 3 else 0)), A.add, col("ex%d" % (n - 1)), A.mult)
 
     for t in range(2):
         X, Q, S = "xi%d" % t, "qx%d" % t, "sx%d" % t
@@ -366,154 +404,168 @@ def rank_program(g, core, T, topo):
         mm(pa, R("qu2", 0, 128), R("su2", 0, 128), R(Q), R(S))
         mm(pv, R("qu2", 128, 256), R("su2", 128, 256), R(Q), R(S))
         mm(R("pr", 1536, 1792), R("qu2", 0, 128), R("su2", 0, 128), R(Q), R(S))
-        act(R("sg1"), pv, F.Sign)
-        act(R("sg2"), R("sg1"), F.Relu)
-        tt(R("dd"), pa, R("maskb"), A.max)
-        scan(R("ow"), R("d0"), R("dd"), A.max, A.min)
-        share = (15, 14) if t == 0 else (15, 14, 13)
-        for m in share:
-            own, e, n = R("ow", 16 * m + 15, 16 * m + 16), m - 12, 16 * m
-            act(R("rl%d" % m, 0, n + 16), R("pr", 1536, 1552 + n), F.Relu, bias=own, scale=-1.0)
-            act(R("cm3", e, 4 * n, 4), R("rl%d" % m, 0, n), F.Sign, accum=R("rs", m, m + 1))
-            act(R("cm3", 4 * n + e, 4 * n + 64, 4), R("rl%d" % m, n, n + 16), F.Sign)
-        tt(R("cme", 0, 1024, 4), pa, R("ow"), A.is_equal)
-        quant(R("qce"), R("sce"), R("cme"))
-        mm(pc, R("qg"), R("sg"), R("qce"), R("sce"), True, False)
-        for m in (13, 12, 11, 10, 9, 8, "q2", 7, 6, 5, 4, "q1", "q3", 3, 2, 1, 0, "q0"):
-            if m in share:
-                continue
-            if isinstance(m, int):
-                a, e = m // 4, m % 4
-                ts(R("cm%d" % a, e, 64 * m + 64, 4), R("pr", 0, 16 * m + 16), R("ow", 16 * m + 15, 16 * m + 16), A.is_lt)
-                if m:
+        plane(X, 0)
+        if t == 0:
+            quant(R("qg"), R("sg"), R("gt"))
+            act(R("dv", 0, 256, 16), R("c16"), F.Identity, bias=col("pf"))
+        else:
+            plane(X, 1)
+        act(R("sgn"), pv, F.Sign, bias=-2.0 ** -120)
+        tt(R("dd"), pa, R("mk"), A.min)
+        scan(R("ow"), R("d0"), R("dd"), A.min, A.max)
+        for m in (15, 14, 13):
+            own, n = R("ow", 16 * m + 15, 16 * m + 16), 16 * m
+            act(R("rl%d" % m, 0, n), R("pr", 1536, 1536 + n), F.Relu, bias=own, scale=-1.0)
+        for m in (15, 14, 13):
+            act(R("cm0", LANE[m][1], 64 * m, 4), R("rl%d" % m, 0, 16 * m), F.Sign, accum=R("rs", m, m + 1))
+        if t == 0:
+            act(R("kc"), R("ek", 0, 256), F.Identity, bias=0.5, scale=EPS)
+            more_iotas()
+        for m in (12, 11, 10, 9, "in", "q1", 8, 7, 6, 5, "v1", "q2", 4, 3, 2, 1, "q0", "q3", "r4", "r3", "r2", "r1", "pay"):
+            if m == "in":
+                tt(R("cm0", 0, 1024, 4), pa, R("ow"), A.is_le)
+            elif m == "v1":
+                scan(R("v1"), R("dv"), R("cm0", 0, 1024, 4), A.max, A.subtract, -64.0)
+            elif m == "pay":
+                scan(R("pay"), R("kc"), R("sgn"), A.max, A.mult)
+            elif isinstance(m, int):
+                a, e = LANE[m]
+                ts(R("cm%d" % a, e, 64 * m, 4), R("pr", 0, 16 * m), R("ow", 16 * m + 15, 16 * m + 16), A.is_lt)
+                if m > 4:
                     act(R("junk", 8 * m * (m - 1), 8 * m * (m + 1)), R("cm%d" % a, e, 64 * m, 4), F.Copy, accum=R("rs", m, m + 1))
+            elif m[0] == "r":
+                m = int(m[1])
+                red(R("rs", m, m + 1), R("cm3", LANE[m][1], 64 * m, 4), A.add)
             else:
                 a = int(m[1])
                 quant(R("qc%d" % a), R("sc%d" % a), R("cm%d" % a))
-                mm(R("pr", 1024, 1024 + WD[a]), R("qg"), R("sg"), R("qc%d" % a), R("sc%d" % a), False, a == 0)
-        planes(X)
-        tt(R("pay"), R("sg2"), R("io20"), A.add)
-        tt(R("rt"), R("rs"), R("c16"), A.subtract)
-        tt(R("dw2"), pc, R("maskb"), A.max)
-        scan(R("ow2"), R("d0"), R("dw2"), A.max, A.min)
-        tt(R("rk"), R("ow2", 15, 256, 16), R("rt"), A.subtract)
-        cp(R("ro"), R("rk"))
-        cp(R("win"), R("pay"), scatter=R("ro"))
-        scan(R("cum"), R("win"), R("ones"), A.add, A.add)
-        ts(col("tm"), R("cum", 255, 256), -0.5, A.add)
-        count(1, 4, col("tm"))
+                mm(R("pr", 1024, 1024 + WD[a]), R("qg"), R("sg"), R("qc%d" % a), R("sc%d" % a), a == 1, a == 3)
         if t == 0:
-            late_constants()
-        tt(R("dw3"), R("win"), R("maskb"), A.max)
-        answer(1, "kc0")
-        edge(1)
-        place(1)
-        ts(R("bs2"), R("cum"), 2.0, A.mult, col("tm"), A.add, off=col("ao1"))
-        count(2, 3, R("bs2", 0, 1))
-        ts(col("kx1"), col("ky1"), col("km1"), A.is_equal, -5000.0, A.mult)
-        tt(col("kcb"), col("kx1"), col("kc0"), A.add)
-        scan(R("ow3"), R("d0"), R("dw3"), A.max, A.min)
-        answer(2, "kcb")
-        edge(2)
-        place(2)
-        ts(R("bs3"), R("cum"), 1.0, A.mult, col("tm"), A.add, off=col("ao2"))
-        count(3, 2, R("bs3", 0, 1))
-        ts(R("bt"), R("ow3", 15, 256, 16), 1.0, A.is_ge)
-        ts(col("kx2"), col("ky2"), col("km2"), A.is_equal, -5000.0, A.mult)
-        tt(R("io"), R("ow3", 15, 256, 16), R("bt"), A.subtract)
-        tt(col("kcc"), col("kx2"), col("kcb"), A.add)
-        ts(R("ol"), R("io"), 2.0 ** 20, A.mult)
-        for b in range(4):
-            act(R("xs", PT * b, PT * b + 256), R("xp", 256 * b, 256 * b + 256), F.Copy, off=R("ol"))
-        ts(R("t1"), R("ck2"), col("km2"), A.is_equal, col("fr1"), A.mult)
-        ts(R("xa"), R("ck1"), col("km1"), A.is_equal, col("e1"), A.mult)
-        ts(R("xb"), R("ck2"), col("km2"), A.is_equal, col("e2"), A.mult)
-        tt(R("t1"), R("t1"), R("s16p"), A.add)
-        tt(R("xa"), R("xa"), R("xb"), A.add)
-        answer(3, "kcc")
-        ts(col("fr3"), col("km3"), -0.125, A.mult, 257.375, A.add)
-        ts(col("em"), col("km3"), -0.125, A.mult, 256.875 - NO, A.add)
-        ts(col("dda"), col("fr3"), -1.0, A.mult, col("fr2"), A.add)
-        ts(R("t3"), R("ck3"), 0.0, A.is_gt, col("fr3"), A.mult)
-        ts(R("en"), R("ck3"), col("km3"), A.is_equal, col("em"), A.mult)
-        ts(R("t2"), R("ck3"), col("km3"), A.is_equal, col("dda"), A.mult)
-        tt(R("t1"), R("t1"), R("t3"), A.add)
-        tt(R("en"), R("en"), R("xa"), A.add)
-        tt(R("t1"), R("t1"), R("t2"), A.add)
-        tt(R("vl"), R("t1"), R("en"), A.is_lt)
-        tt(R("plf"), R("t1"), R("vl"), A.mult)
-        ts(R("pl"), R("plf"), float(NO), A.add)
-        for o, lo, q, s in (("b13", 0, "qb%d" % t, "sb%d" % t), ("b02", 8, "wbc%d" % t, "wbs%d" % t)):
-            for b in (2, 0, 3, 1):
-                if b < 2:
-                    cp(R(o, b, 512, 4), R("xs", PT * b, PT * b + PT), off=R("pl", lo, lo + 8))
-                else:
-                    act(R(o, b, 512, 4), R("xs", PT * b, PT * b + PT), F.Copy, off=R("pl", lo, lo + 8))
-            quant(R(q, 0, 128), R(s, 0, 128), R(o))
+            ts(R("dx"), R("jm"), col("p4m"), A.add, -300.0, A.max)
+            scan(R("mx"), R("z16"), R("mk"), A.min, A.max)
+            ts(R("dx", 15, 256, 16), R("dx", 15, 256, 16), 8192.0, A.add)
+            tail_constants()
+            plane(X, 1)
+        plane(X, 2)
+        plane(X, 3)
+        scan(R("exr"), pc, R("dx"), A.max, A.subtract)
+        tt(R("rt"), R("v1", 15, 256, 16), R("rs"), A.subtract)
+        tt(R("rk"), R("exr", 15, 256, 16), R("rt"), A.add)
+        ts(R("ro"), R("rk"), col("cro"), A.add)
+        cp(R("win"), R("pay"), scatter=R("ro"))
+        scan(R("cum", 2, 514, 2), R("win"), R("c15"), A.add, A.add, 0.125)
+        all_ = R("cum", 512, 513)
+        count(1, all_)
+        scan(R("exw"), R("win"), R("mx"), A.add, A.mult)
+        tt(R("sq"), R("exw", 15, 256, 16), R("exw", 15, 256, 16), A.mult)
+        answer(1)
+        ts(R("ol"), R("sq"), 2.0 ** 82, A.mult, -2.0 ** 20, A.add)
+        ts(R("g1"), R("cum", 0, 512), 2.0 - 2.0 ** -8, A.mult, all_, A.add, off=col("id1"))
+        tt(R("key1"), R("ek"), R("kfr"), A.add, off=col("id1"))
+        red(col("bs1"), R("g1"), A.min)
+        xs = [lambda b=b: act(R("xs", PT * b, PT * b + 256), R("xp", 512 * b, 512 * b + 256), F.Copy, off=R("ol")) for b in range(4)]
+        count(2, col("bs1"))
+        xs[0]()
+        red(col("km1"), R("key1"), A.min)
+        tt(R("m1"), R("s2"), R("key1"), A.max)
+        ts(col("ex1"), col("id1"), col("kfo"), A.add, col("km1"), A.is_gt)
+        ts(R("f2"), R("s2"), col("km1"), A.add)
+        answer(2)
+        ts(R("ii", 0, 32, 2), R("m1"), col("km1"), A.is_gt)
+        ts(R("g2"), R("cum", 0, 512), 1.0 - 2.0 ** -9, A.mult, all_, A.add, off=col("id2"))
+        tt(R("key2"), R("ek"), R("kfr"), A.add, off=col("id2"))
+        red(col("bs2"), R("g2"), A.min)
+        count(3, col("bs2"))
+        for b in (1, 2, 3):
+            xs[b]()
+        red(col("km2"), R("key2"), A.min)
+        tt(R("m2"), R("f2"), R("key2"), A.max)
+        ts(col("ex2"), col("id2"), col("kfo"), A.add, col("km2"), A.is_gt)
+        ts(R("ff", 1, 32, 2), R("f2"), U9, A.mult)
+        answer(3)
+        ts(R("gg", 1, 32, 2), R("s2"), col("km2"), A.add, U9, A.mult)
+        tt(R("key3"), R("ek3"), R("kfr9"), A.add, off=col("id3"))
+        tt(R("kn3"), R("ek3n"), R("kfr9"), A.add, off=col("id3"))
+        red(col("km3"), R("key3"), A.min)
+        tt(R("m3"), R("gg", 1, 32, 2), R("key3"), A.max)
+        ts(R("ii", 1, 32, 2), R("m2"), col("km2"), A.is_gt)
+        ts(R("hh", 0, 32, 2), R("kn3"), col("km3"), A.is_le, col("km3"), A.add)
+        ts(R("hh", 1, 32, 2), R("m3"), col("km3"), A.is_gt)
+        tt(R("qq", 1, 64, 2), R("ii"), R("ff"), A.add)
+        tt(R("qq", 0, 64, 2), R("hh"), R("gg"), A.add)
+        scan(R("qo"), R("d4"), R("qq"), A.max, A.min)
+        ts(R("pl"), R("qo", 3, 64, 4), 256.0, A.mult)
+        for o, lo, q, s, at in (("b13", 0, "qb%d" % t, "sb%d" % t, 0), ("b02", 8, "wbc%d" % t, "wbs%d" % t, 64)):
+            for b in (0, 2, 1, 3):
+                pick("v" if b < 2 else "s", R(o, b, 512, 4), R("xs", PT * b, PT * b + PT), R("pl", lo, lo + 8))
+            quant(R(q, at, at + 128), R(s, at, at + 128), R(o))
             if lo == 0:
                 send_two("b", "c", q, t)
                 send_two("b", "s", s, t)
         d2 = T.cores[(rank + 2) % N]
-        send_one("b", "c", "wbc%d" % t, 0, d2, 128, "wbc%d" % t, t)
-        send_one("b", "s", "wbs%d" % t, 0, d2, 128, "wbs%d" % t, t)
+        send_one("b", "c", "wbc%d" % t, 128, d2, 0, t)
+        send_one("b", "s", "wbs%d" % t, 128, d2, 0, t)
         for b in range(4):
             for k in range(2):
                 act(R("e2x", 128 * b + 64 * k, 128 * b + 64 * k + 64), R("xs", PT * b, PT * b + 64), F.Copy, scale=0.5)
         if t == 0:
-            for b in range(4):
-                quant(R("qe%d" % b), R("se%d" % b), R("ex", 3 - b, 515 - b))
-        lands("adb%d" % t, 16, [R("wbc%d" % t, 128, 192), R("wbs%d" % t, 128, 192)])
+            act(R("eh"), R("ex"), F.Copy, scale=0.5)
+            late_constants()
+        lands("adb%d" % t, 16, [R("wbc%d" % t, 0, 64), R("wbs%d" % t, 0, 64)])
         lands("aob%d" % t, 32, [R("lbc%d" % t), R("lbs%d" % t)])
-        layer("wbc%d" % t, "wbs%d" % t, 64, "za", "qza", "sza", "ha", "whc%d" % t, "whs%d" % t, 64)
-        p2 = T.cores[(rank - 2) % N]
-        send_one("h", "c", "whc%d" % t, 128, p2, 0, "whc%d" % t, t)
-        send_one("h", "s", "whs%d" % t, 128, p2, 0, "whs%d" % t, t)
-        layer("lbc%d" % t, "lbs%d" % t, 0, "zb", "qzb", "szb", "hb", "qh%d" % t, "sh%d" % t, 0)
+        unpack("pr", "e", "wbc%d" % t, "wbs%d" % t, 0)
+        mix("pr", "za")
+        unpack("pd", "e", "lbc%d" % t, "lbs%d" % t, 0)
+        mix("pd", "zb")
+        layer("pr", "zb")
+        layer("pd", "za")
+        scaled("pr", "hb", "qh%d" % t, "sh%d" % t)
         send_two("h", "c", "qh%d" % t, t)
         send_two("h", "s", "sh%d" % t, t)
+        scaled("pd", "ha", "whc%d" % t, "whs%d" % t)
+        p2 = T.cores[(rank - 2) % N]
+        send_one("h", "c", "whc%d" % t, 0, p2, 128, t)
+        send_one("h", "s", "whs%d" % t, 0, p2, 128, t)
         if t == 0:
             later_constants()
-        place(3)
-        for n in (1, 2, 3):
-            ts(col("af%d" % n), col("ao%d" % n), 1.0, A.add)
-            ts(R("w%d" % n), R("ck%d" % n), col("km%d" % n), A.is_equal)
-            tt(R("c%d" % n), R("w%d" % n), R("k16"), A.mult)
-            red(col("cb%d" % n), R("c%d" % n), A.add)
-        tt(col("cb4"), col("cb1"), col("cb2"), A.add)
-        tt(col("cb4"), col("cb4"), col("cb3"), A.add)
-        ts(col("cb4"), col("cb4"), -1.0, A.mult, 384.0, A.add)
-        for n in (2, 3, 4):
-            tt(col("db%d" % n), col("cb%d" % n), col("cb%d" % (n - 1)), A.subtract)
-        tt(col("da2"), col("af2"), col("af1"), A.subtract)
-        tt(col("da3"), col("af3"), col("af2"), A.subtract)
-        for n, d in ((1, "af1"), (2, "da2"), (3, "da3")):
-            ts(R("y%d" % n), R("rk"), col("af%d" % n), A.is_ge, col(d), A.mult)
-            ts(R("z%d" % n), R("rk"), col("af%d" % n), A.is_ge, col("db%d" % (n + 1)), A.mult)
-        tt(R("rl"), R("rk"), R("y1"), A.subtract)
-        tt(R("rl"), R("rl"), R("y2"), A.subtract)
-        tt(R("rl"), R("rl"), R("y3"), A.subtract)
-        ts(R("sv1"), R("rl"), col("cb1"), A.add, -256.0, A.add)
-        for n in (1, 2, 3):
-            tt(R("sv1"), R("sv1"), R("z%d" % n), A.add)
-        ts(R("vl"), R("rl"), 64.0, A.is_lt)
-        tt(R("sf"), R("sv1"), R("vl"), A.mult)
-        ts(R("so"), R("sf"), 256.0, A.add)
+        ts(R("ft"), R("pl", 0, 16, 4), col("pfm"), A.subtract)
+        ts(R("r1"), R("ro"), 1.0, A.add)
+        tt(R("ft2"), R("ft"), R("fr4"), A.subtract)
+        for c in range(4):
+            ts(R("uu", c, 64, 4), R("r1"), R("ft2", c, c + 1), A.is_ge, R("ft2", c, c + 1), A.mult)
+        scan(R("uo"), R("z4"), R("uu"), A.min, A.max)
+        tt(R("w"), R("r1"), R("uo", 3, 64, 4), A.subtract)
+        cp(R("ri"), R("w"))
+        ts(R("sb"), R("w"), 512.0, A.mult)
+        ts(R("st"), R("w"), 64.0, A.is_ge, -4096.0, A.mult)
+        ts(R("sa"), R("ri"), -511.0, A.mult, 256.0, A.add)
+        tt(R("sb"), R("sb"), R("st"), A.add)
+        tt(R("sa"), R("sa"), R("sb"), A.add)
+        tt(R("sa"), R("sa"), R("cj"), A.max)
+        cp(R("so"), R("sa"))
         if t == 1:
             act(R("slr"), R("tb"), F.Copy, off=R("so"))
             dma("y", T.sl[:], T.slr[0:128:16, :], (), [R("slr")])
-        lands("adh%d" % t, 16, [R("whc%d" % t, 0, 64), R("whs%d" % t, 0, 64)])
+        lands("adh%d" % t, 16, [R("whc%d" % t, 128, 192), R("whs%d" % t, 128, 192)])
         lands("aoh%d" % t, 32, [R("lhc%d" % t), R("lhs%d" % t)])
-        unpack("whc%d" % t, "whs%d" % t, 0, 128)
-        unpack("lhc%d" % t, "lhs%d" % t, 0, 0)
+        unpack("pr", "f", "whc%d" % t, "whs%d" % t, 64)
+        renew("pr", "b02", 384)
+        unpack("pd", "f", "lhc%d" % t, "lhs%d" % t, 0)
+        renew("pd", "b13", 256)
         X2 = "xi%d" % (t + 1)
-        for b in range(4):
-            tt(R(X2, b, 1024, 4), R("dwn", PD * b, PD * b + PD), R(X, b, 1024, 4), A.add, off=R("so"))
-        quant(R("qx%d" % (t + 1)), R("sx%d" % (t + 1)), R(X2))
-    mm(R("pr", 0, 256), R("qv"), R("sv"), R("qx2"), R("sx2"))
+        for q, b, lo, hi in (("s", 0, 0, 16), ("s", 1, 0, 16), ("v", 3, 0, 16), ("s", 2, 0, 8), ("v", 2, 8, 16)):
+            pick(q, R(X2, b + 64 * lo, 64 * hi, 4), R("xp", 512 * b, 512 * b + 512), R("so", lo, hi))
+        if t == 0:
+            quant(R("qx1"), R("sx1"), R(X2))
+    for h in range(2):
+        a, b = 128 * h, 128 * h + 128
+        quant(R("qx2", a, b), R("sx2", a, b), R("xi2", 4 * a, 4 * b))
+        mm(bank("pr", h), R("qv"), R("sv"), R("qx2", a, b), R("sx2", a, b))
     dma("y", T.oc[:], ap(R("qx2")).bitcast(dt.uint8), (), [R("qx2")])
     for k in range(4):
         dma("s" if k % 2 else "y", T.osc[4 * k:4 * k + 4, :], T.sx2[32 * k:32 * k + 4, :], (), [R("sx2")])
-    act(R("ycp"), R("pr", 0, 256), F.Copy)
+    for h in range(2):
+        cp(R("ycp", 128 * h, 128 * h + 128), bank("pr", h))
     dma("s", T.y[:], ap(R("ycp")), (), [R("ycp")])
     tot["loc"] = nloc[0]
     for sem in sorted(tot):

@@ -4,11 +4,18 @@ from concourse.mybir import dt, AluOpType as A, AxisListType, ActivationFunction
 N = 8
 C = 256
 PT = 320
-WD = (256, 256, 128, 128)
-LANE = {15: (0, 1), 14: (0, 2), 13: (0, 3)}
-LANE.update({m: (1 + (12 - m) // 4, (12 - m) % 4) for m in range(1, 13)})
-EPS = 2.0 ** -22
-U9 = 2.0 ** -9
+WD = (240, 256, 128, 128)
+LANE = {15: (0, 0), 14: (0, 1), 13: (0, 2), 12: (0, 3), "in": (1, 0), 11: (1, 1), 10: (1, 2), 9: (1, 3)}
+LANE.update({m: (2 + (8 - m) // 4, (8 - m) % 4) for m in range(1, 9)})
+SHARE = (15, 14, 13)
+ORDER = ("lo 12 lo2 sgn qg 11 10 9 a12 8 in a11 a10 6 7 mf a9 5 v1 q1 a7 1 q2 a8 2 3 4 a6 q0 q3 r1 r5 r3 rk r2 r4 rt pay exr tc all p0 p1 p2 p3 ro",
+         "lo 12 lo2 10 11 in 9 a9 8 a10 a12 a11 q1 7 6 a6 5 a7 2 3 v1 4 q2 1 a8 q0 q3 rk r4 sgn r3 r5 r1 r2 all rt exr pay p2 p3 ro")
+CUTS = ("c1 exw cum id1 g1 key1 bs1 c2 sq km1 m1 ol ex1 x0 ff id2 ii0 g2 key2 bs2 c3 km2 m2 ex2 gg1 x1 x2 x3 ii1 id3 y1 key3 kn3 km3 m3 y2 "
+        "gg0 hh0 hh2 hh1 min pl")
+STEPS = ("Ua0123 Ma0123 Qa Ub0123 Wa20 Mb0123 Qb Wb2031 Wa31 Hb Ha", "Ua01 Ma01 Ub0123 Mb0123 Ua23 Qb Wb2031 Ma23 Qa Wa2031 Hb Ha")
+BACK = "a0 a1 a2 a3 b0 b1 b2 b3"
+PICKS = (("s", 0, 0, 16), ("s", 1, 0, 16), ("v", 2, 8, 16), ("v", 3, 0, 16), ("s", 2, 0, 8), ("q", 1, 8, 16), ("q", 0, 0, 8))
+ONE = 2 ** 21
 SCRATCH = {}
 PLACE = {}
 PSUM = ("pr", "pd")
@@ -24,6 +31,7 @@ def _spans():
 
 SPAN = _spans()
 E3, EK = 2 * SPAN[2][0], 2 * SPAN[2][1] + 2
+CW = 2 * SPAN[1][1] + 2
 
 
 def _decl():
@@ -47,18 +55,18 @@ def _decl():
     add("qu2", 256, q), add("su2", 256, s)
     add("wq", 512, q), add("wsc", 512, s)
     share("ci", i, ("iP pq pb2 pb3 pg", 2))
-    share("cfl", f, ("jm ab mk d0 z16 dx mx kc c15", 256), ("ek", EK), ("ek3 ek3n", EK - E3 + 8), ("tb", 512),
-          ("pf k1 kf kfo gpf p4 p4m cro pfm", 2), ("iL", 8), ("c16 kq kfr kfr9 s1 s2 cj", 16), ("fr4", 4), ("d4 z4", 64))
+    share("cfl", f, ("jm ab mk d0 z16 mx kc c3", 256), ("ek", EK), ("ek3 ek3n", EK - E3 + 8), ("tb", 512),
+          ("pf k1 kf kfo gpf p4 pf1 pfm p4m cro c0", 2), ("iL", 8), ("c16 kq kfr s1 cj d15", 16), ("fr4 fr8", 4), ("z4", 64))
     add("ul", 16, h)
-    add("gt iC", 512, b), add("hf ex eh", 516, b), add("dv", 256, b)
+    add("gt", 512, b), add("iC", 128, b), add("hf ex eh", 516, b), add("dv", 256, b)
     share("qk", q, ("qg qe0 qe1 qe2 qe3 qf0 qf1 qf2 qf3", 128)), share("sk", s, ("sg se0 se1 se2 se3 sf0 sf1 sf2 sf3", 128))
     for k in range(4):
         add("cm%d" % k, 4 * WD[k], b)
     share("qc", q, *[("qc%d" % k, WD[k]) for k in range(4)]), share("sc", s, *[("sc%d" % k, WD[k]) for k in range(4)])
-    add("dd ow sgn pay exr win exw ycp slr", 256, f), add("cum", 520, f), add("v1", 256, b)
+    add("dx dd ow sgn pay exr win exw ycp slr", 256, f), add("cum", 520, f), add("v1", 256, b)
     add("junk", 1920, b), add("junk2", 384, b), add("rl13 rl14 rl15", 256, b)
-    share("sm", f, ("rs rt rk sq g1 g2 key1 key2 key3 kn3 m1 m2 m3 f2 r1 w sa sb st", 16), ("ii ff gg hh", 32), ("qq qo uu uo", 64),
-          ("ac1 ac2 ac3 bs1 bs2 km1 km2 km3 ex1 ex2", 2), ("ft ft2", 4))
+    share("sm", f, ("rs rk sq g1 g2 key1 key2 key3 kn3 m1 m2 m3 r1 w sa sb st", 16), ("ii ff", 32), ("uu uo", 64), ("qa qb qo", 96),
+          ("ac1 ac2 ac3 bs1 bs2 km1 km2 km3 ex1 ex2 sgs all", 2), ("ft ft2", 4))
     share("li", h, ("ro pl so ol ri", 16), ("id1 id2 id3", 2))
     add("xp", 2048, b), add("xs", 4 * PT, b), add("e2x", 512, b)
     add("b13 b02 za zb ha hb", 512, b), add("qza qzb", 128, q), add("sza szb", 128, s)
@@ -72,7 +80,7 @@ def _decl():
 
 
 _decl()
-SEMAPHORES = ["ev", "es", "et", "eg", "loc"] + ["d%d" % k for k in range(14)] + [
+SEMAPHORES = ["ev", "es", "et", "eg", "loc"] + ["d%d" % k for k in range(21)] + [
     "%s%s%d" % (a, b, t) for a in ("rc", "rs", "ao", "ad") for b in "bh" for t in range(2)]
 
 
@@ -202,7 +210,9 @@ def rank_program(g, core, T, topo):
         op("v", [out], [i] + [o for o in (off, scatter) if o], lambda e: e.tensor_copy(out=dst, in_=src))
 
     def scan(out, a, b, o0, o1, first=0.0):
-        op("v", [out], [a, b], lambda e: e.tensor_tensor_scan(out=ap(out), data0=ap(a), data1=ap(b), initial=first, op0=o0, op1=o1))
+        at = isinstance(first, tuple)
+        op("v", [out], [a, b] + [first] * at,
+           lambda e: e.tensor_tensor_scan(out=ap(out), data0=ap(a), data1=ap(b), initial=ap(first) if at else first, op0=o0, op1=o1))
 
     def red(out, i, o):
         op("v", [out], [i], lambda e: e.tensor_reduce(out=ap(out), in_=ap(i), axis=AxisListType.X, op=o))
@@ -247,87 +257,101 @@ def rank_program(g, core, T, topo):
     def plane(x, b):
         act(R("xp", 512 * b, 512 * b + 256), R(x, b, 1024, 4), F.Copy)
 
+    def nought(m):
+        a, e = LANE[m]
+        iota(R("cm%d" % a, 64 * m + e, 4 * WD[a], 4), [[0, WD[a] - 16 * m]], 0, 0)
+
+    dma("y", ap(R("ub")), T.u[:], [R("ub")])
     dma("y", ap(R("xi0")), T.x[:], [R("xi0")])
-    dma("s", ap(R("ub")), T.u[:], [R("ub")])
+    fill(R("cm3", 64), 0.0)
+    fill(R("dv"), -64.0)
     iota(R("iP"), [[0, 2]], 0, 1, False)
-    iota(R("jm"), [[0, 16], [-4096, 16]], 0, 0)
     iota(R("iL"), [[16, 8]], 0, 0)
-    iota(R("kq"), [[-1, 2], [2, 2], [0, 4]], 1, 0)
-    iota(R("s1"), [[0, 4], [32, 4]], 0, 0)
-    iota(R("iC"), [[1, 8], [0, 64]], 0, 0)
+    iota(R("jm"), [[0, 16], [-4096, 16]], 0, 0)
+    iota(R("iC"), [[1, 8], [0, 16]], 0, 0)
+    iota(R("z16"), [[0, 256]], 1, 0)
+    iota(R("z16", 0, 256, 16), [[0, 16]], 0, 0)
+    for m in (9, 10, 11):
+        nought(m)
+    iota(R("dv", 0, 256, 16), [[16, 16]], 15, 0)
+    for m in (12, 13, 14):
+        nought(m)
+    iota(R("kc"), [[1, 256]], ONE, 0)
     iota(R("c16"), [[16, 16]], 15, 0)
     iota(R("rs", 0, 1), [[0, 1]], 0, 0)
-    iota(R("ek"), [[1, EK]], 0, 0)
-    iota(R("cum"), [[0, 520]], 4096, 0)
-    iota(R("d4"), [[0, 16], [-64, 4]], 64, 0)
-    for b in range(4):
-        iota(R("xs", PT * b + 256, PT * b + PT), [[0, PT - 256]], 0, 0)
+    iota(R("kq"), [[-1, 2], [2, 2], [0, 4]], 1, 0)
+    iota(R("s1"), [[0, 4], [32, 4]], 0, 0)
+    iota(R("c3"), [[0, 256]], 3 * ONE, 0)
+    iota(R("ek", 8), [[1, EK - 8]], 8, 0)
+    iota(R("ek", 0, 8), [[0, 8]], 4096, 0)
+    iota(R("qa"), [[0, 96]], 0, 0)
+    iota(R("qa", 0, 96, 6), [[0, 16]], 4096, 0)
+    iota(R("qb"), [[0, 96]], 4096, 0)
+    iota(R("ek3", 0, 8), [[0, 8]], 4096, 0)
+    iota(R("ek3n", 0, 8), [[0, 8]], -1, 0)
 
     def more_iotas():
-        iota(R("ek", 0, 8), [[0, 8]], 4096, 0)
-        iota(R("ek3", 0, 8), [[0, 8]], 64, 0)
-        iota(R("ek3n", 0, 8), [[0, 8]], -1, 0)
         iota(R("hf"), [[0, 516]], 1, 0)
         select(R("ex"), R("hf"), [[-1, 516]], A.is_equal, 0.0, 3, 4)
         iota(R("fr4"), [[1, 4]], 0, 0)
         iota(R("z4"), [[0, 16], [4096, 4]], 0, 0)
+
+    def last_iotas():
         iota(R("tb", 0, 256), [[0, 256]], -1, 0)
         iota(R("tb", 256, 384), [[128, 2], [1, 64]], 64, 0)
         iota(R("tb", 384, 512), [[128, 2], [1, 64]], 0, 0)
-    for a, lo in enumerate((208, 144, 80, 16)):
-        fill(R("cm%d" % a, 4 * lo, 4 * WD[a]), 0.0)
-    fill(R("dv"), -64.0)
     ts(R("pq"), R("iP"), 15, A.bitwise_and)
     ts(R("pb2"), R("iP"), 2, A.arith_shift_right, 1, A.bitwise_and)
     ts(R("pb3"), R("iP"), 3, A.arith_shift_right, 1, A.bitwise_and)
-    ts(R("p4"), R("pq"), 4096.0, A.mult)
-    ts(R("k1"), R("pb2"), 2.0, A.mult, 1.0, A.add)
     ts(R("pg"), R("iP"), 4, A.arith_shift_right)
-    tt(R("kf"), R("k1"), R("pb3"), A.subtract)
-    ts(R("p4m"), R("pq"), 4096.0, A.mult, -300.0, A.add)
-    cp(R("gpf"), R("pg"))
     ts(R("pf"), R("pq"), -1.0, A.mult)
-    ts(R("cro"), R("pq"), 300.0, A.mult, 3392.0, A.add)
+    ts(R("k1"), R("pb2"), 2.0, A.mult, 1.0, A.add)
+    cp(R("gpf"), R("pg"))
+    tt(R("kf"), R("k1"), R("pb3"), A.subtract)
     ts(R("ul", 0, 8), R("iL"), 4.0, A.add)
     ts(R("ul", 8, 16), R("iL"), col("kf"), A.add)
+    act(R("p4"), R("pf"), F.Copy, scale=-4096.0)
     act(R("ab"), R("jm"), F.Abs, bias=col("p4"))
-    act(R("d0"), R("jm"), F.Identity, bias=-2.0 ** 91, scale=-2.0 ** 80)
     act(R("mk"), R("ab"), F.Identity, bias=2.0 ** 91, scale=-2.0 ** 80)
-    ts(R("pfm"), R("pq"), 2.0, A.mult, 0.5, A.add)
     quant(R("qu"), R("su"), R("ub"))
     op("v", [R("qu2")], [R("qu"), R("ul")],
        lambda e: e.tensor_copy(ap(R("qu2")).bitcast(dt.uint32), ap(R("qu")).bitcast(dt.uint32).indirect(ap(R("ul")))))
     act(R("su2"), R("su"), F.Copy, off=R("ul"))
+    act(R("d0"), R("jm"), F.Identity, bias=-2.0 ** 91, scale=-2.0 ** 80)
     quant(R("qx0"), R("sx0"), R("xi0"))
-    act(R("z16"), R("jm"), F.Sign, scale=-1.0)
+    for e in range(4):
+        ts(R("gt", e, 512, 4), R("iC"), col("gpf"), A.is_equal)
+    scan(R("mx"), R("z16"), R("mk"), A.min, A.max)
     before("y", (), [R("xi0")], "dma")
+    for to in [R("cm2", 320)] + [R("xs", PT * b + 256, PT * b + PT) for b in range(4)]:
+        zero = R("cm3", 256, 256 + to[2] - to[1])
+        dma("y", ap(to), ap(zero), [to], [zero])
+    dma("y", ap(R("cum", 4, CW)), ap(R("jm", 0, CW - 4)), [R("cum", 4, CW)], [R("jm", 0, CW - 4)])
     dma("y", ap(R("wq")).bitcast(dt.uint8), T.wc[:], [R("wq")])
     dma("y", ap(R("wsc")), T.ws[:], [R("wsc")])
     dma("y", ap(R("vb")), T.v[:], [R("vb")])
-    ts(R("gt"), R("iC"), col("gpf"), A.is_equal)
+    for k in ("ek3", "ek3n"):
+        dma("y", ap(R(k, 8)), ap(R("ek", E3, EK)), [R(k, 8)], [R("ek", E3, EK)])
+    s2 = R("ff", 0, 32, 2)
 
     def tail_constants():
-        act(R("c15"), R("jm"), F.Identity, bias=1.5, scale=0.0)
-        act(R("mx", 15, 256, 16), R("mx", 15, 256, 16), F.Copy, scale=2.0 ** -121)
+        act(R("cum", 0, 4), R("c16", 0, 4), F.Identity, bias=4096.0 * ONE, scale=0.0)
+        act(R("pfm"), R("pf"), F.Identity, bias=0.5, scale=-2.0)
         act(R("kfr"), R("kq"), F.Copy, scale=0.0625)
         act(R("kfo"), R("kf"), F.Copy, scale=0.0625)
-        act(R("s2"), R("s1"), F.Identity, bias=col("pfm"))
-        act(R("kfr9"), R("kq"), F.Copy, scale=0.0625 * U9)
-        act(R("ff", 0, 32, 2), R("s2"), F.Copy, scale=U9)
-        act(R("gg", 0, 32, 2), R("s2"), F.Copy, scale=U9)
-        act(R("ek3", 8), R("ek", E3, EK), F.Copy, scale=U9)
-        act(R("ek3n", 8), R("ek", E3, EK), F.Copy, scale=U9)
+        act(s2, R("s1"), F.Identity, bias=col("pfm"))
 
     def late_constants():
+        act(R("eh"), R("ex"), F.Copy, scale=0.5)
+        act(R("pf1"), R("pf"), F.Identity, bias=1.0)
+        act(R("fr8"), R("fr4"), F.Copy, scale=0.125)
+        ts(R("cj"), R("c16"), col("pf"), A.subtract, -15.0, A.add)
         for b in range(4):
             quant(R("qe%d" % b), R("se%d" % b), R("eh", 3 - b, 515 - b))
 
     def later_constants():
         for b in range(4):
             quant(R("qf%d" % b), R("sf%d" % b), R("ex", 3 - b, 515 - b))
-        ts(R("pfm"), R("pq"), -1.0, A.add)
-        ts(R("fr4"), R("fr4"), 0.125, A.mult)
-        ts(R("cj"), R("c16"), col("pf"), A.subtract, -15.0, A.add)
         quant(R("qv"), R("sv"), R("vb"))
 
     rel = {(w, i): d for d, w, i in _relays(topo, T.cores, rank)}
@@ -361,18 +385,8 @@ def rank_program(g, core, T, topo):
     def bank(ps, b):
         return R(ps, 512 * b, 512 * b + 128)
 
-    def unpack(ps, e, q, s, off):
-        for b in range(4):
-            mm(bank(ps, b), R("q%s%d" % (e, b)), R("s%s%d" % (e, b)), R(q, off, off + 128), R(s, off, off + 128))
-
-    def mix(ps, z):
-        for b in range(4):
-            tt(R(z, b, 512, 4), bank(ps, b), R("e2x", 128 * b, 128 * b + 128), A.add)
-        quant(R("q" + z), R("s" + z), R(z))
-
-    def layer(ps, z):
-        for b in (2, 0, 3, 1):
-            mm(bank(ps, b), R("wq", 128 * b, 128 * b + 128), R("wsc", 128 * b, 128 * b + 128), R("q" + z), R("s" + z))
+    def unpack(ps, e, q, s, off, b):
+        mm(bank(ps, b), R("q%s%d" % (e, b)), R("s%s%d" % (e, b)), R(q, off, off + 128), R(s, off, off + 128))
 
     def scaled(ps, h, qh, sh):
         for b in (2, 0, 3, 1):
@@ -381,10 +395,6 @@ def rank_program(g, core, T, topo):
             else:
                 act(R(h, b, 512, 4), bank(ps, b), F.Copy, scale=0.03125)
         quant(R(qh, 0, 128), R(sh, 0, 128), R(h))
-
-    def renew(ps, old, to):
-        for b in range(4):
-            tt(R("xp", 512 * b + to, 512 * b + to + 128), bank(ps, b), R(old, b, 512, 4), A.add)
 
     def count(n, bias):
         lo, hi = SPAN[n - 1]
@@ -398,103 +408,118 @@ def rank_program(g, core, T, topo):
         else:
             ts(col("id%d" % n), col("ac%d" % n), float(lo + hi - (E3 - 8 if n == 3 else 0)), A.add, col("ex%d" % (n - 1)), A.mult)
 
+    def placed(b):
+        act(R("xs", PT * b, PT * b + 256), R("xp", 512 * b, 512 * b + 256), F.Copy, off=R("ol"))
+
     for t in range(2):
         X, Q, S = "xi%d" % t, "qx%d" % t, "sx%d" % t
-        pa, pv, pc = R("pr", 0, 256), R("pr", 512, 768), R("pr", 1024, 1280)
+        pa, ps, pv, pc = R("pr", 0, 256), R("pr", 1536, 1792), R("pr", 512, 768), R("pr", 1024, 1280)
         mm(pa, R("qu2", 0, 128), R("su2", 0, 128), R(Q), R(S))
+        mm(ps, R("qu2", 0, 128), R("su2", 0, 128), R(Q), R(S))
         mm(pv, R("qu2", 128, 256), R("su2", 128, 256), R(Q), R(S))
-        mm(R("pr", 1536, 1792), R("qu2", 0, 128), R("su2", 0, 128), R(Q), R(S))
-        plane(X, 0)
         if t == 0:
-            quant(R("qg"), R("sg"), R("gt"))
-            act(R("dv", 0, 256, 16), R("c16"), F.Identity, bias=col("pf"))
+            act(R("p4m"), R("pf"), F.Identity, bias=-2048.0, scale=-4096.0)
+            act(R("c0"), R("pf"), F.Square, bias=16.0)
+            act(R("dx"), R("jm"), F.Identity, bias=col("p4m"))
+            act(R("cro"), R("c0"), F.Identity, bias=col("pf"), scale=-2048.0)
+            act(R("d15"), R("dx", 15, 256, 16), F.Identity, bias=2.0 ** 20)
+            act(R("cro"), R("cro"), F.Identity, bias=2.0 ** 20)
         else:
+            plane(X, 0)
             plane(X, 1)
-        act(R("sgn"), pv, F.Sign, bias=-2.0 ** -120)
-        tt(R("dd"), pa, R("mk"), A.min)
-        scan(R("ow"), R("d0"), R("dd"), A.min, A.max)
-        for m in (15, 14, 13):
-            own, n = R("ow", 16 * m + 15, 16 * m + 16), 16 * m
-            act(R("rl%d" % m, 0, n), R("pr", 1536, 1536 + n), F.Relu, bias=own, scale=-1.0)
-        for m in (15, 14, 13):
-            act(R("cm0", LANE[m][1], 64 * m, 4), R("rl%d" % m, 0, 16 * m), F.Sign, accum=R("rs", m, m + 1))
+        top = 128 if t else 192
+        tt(R("dd", top, 256), bank("pd", 0) if t else R("pr", top, 256), R("mk", top, 256), A.min)
+        scan(R("ow", top, 256), R("d0", top, 256), R("dd", top, 256), A.min, A.max)
+        for m in SHARE:
+            act(R("rl%d" % m, 0, 16 * m), R("pr", 1536, 1536 + 16 * m), F.Relu, bias=R("ow", 16 * m + 15, 16 * m + 16), scale=-1.0)
+        for m in (SHARE[1], SHARE[0], SHARE[2]):
+            act(R("cm%d" % LANE[m][0], LANE[m][1], 64 * m, 4), R("rl%d" % m, 0, 16 * m), F.Sign, accum=R("rs", m, m + 1))
         if t == 0:
-            act(R("kc"), R("ek", 0, 256), F.Identity, bias=0.5, scale=EPS)
             more_iotas()
-        for m in (12, 11, 10, 9, "in", "q1", 8, 7, 6, 5, "v1", "q2", 4, 3, 2, 1, "q0", "q3", "r4", "r3", "r2", "r1", "pay"):
-            if m == "in":
-                tt(R("cm0", 0, 1024, 4), pa, R("ow"), A.is_le)
+        for m in ORDER[t].split():
+            if m == "qg":
+                quant(R("qg"), R("sg"), R("gt"))
+            elif m == "mf":
+                ts(R("mx", 15, 256, 16), R("mx", 15, 256, 16), 2.0 ** -121, A.mult)
+            elif m == "sgn":
+                act(R("sgn"), pv, F.Sign, bias=-2.0 ** -120, accum=col("sgs"))
+            elif m == "all":
+                act(col("all"), col("sgs"), F.Identity, bias=3.0 * C * ONE, scale=float(ONE))
+            elif m == "tc":
+                tail_constants()
+            elif m in ("p0", "p1", "p2", "p3"):
+                plane(X, int(m[1]))
+            elif m == "exr":
+                scan(R("exr"), pc, R("dx"), A.max, A.subtract)
+            elif m == "rk":
+                tt(R("rk"), R("d15"), R("v1", 15, 256, 16), A.subtract)
+            elif m == "rt":
+                tt(R("dx", 15, 256, 16), R("rk"), R("rs"), A.add)
+            elif m == "ro":
+                ts(R("ro"), R("exr", 15, 256, 16), col("cro"), A.add)
+            elif m == "lo":
+                tt(R("dd", 0, top), R("pr", 0, top), R("mk", 0, top), A.min)
+            elif m == "lo2":
+                scan(R("ow", 0, top), R("d0", 0, top), R("dd", 0, top), A.min, A.max)
+            elif m == "in":
+                tt(R("cm1", 0, 1024, 4), pa, R("ow"), A.is_le)
             elif m == "v1":
-                scan(R("v1"), R("dv"), R("cm0", 0, 1024, 4), A.max, A.subtract, -64.0)
+                scan(R("v1"), R("dv"), R("cm1", 0, 1024, 4), A.max, A.subtract, -64.0)
             elif m == "pay":
                 scan(R("pay"), R("kc"), R("sgn"), A.max, A.mult)
-            elif isinstance(m, int):
-                a, e = LANE[m]
-                ts(R("cm%d" % a, e, 64 * m, 4), R("pr", 0, 16 * m), R("ow", 16 * m + 15, 16 * m + 16), A.is_lt)
-                if m > 4:
-                    act(R("junk", 8 * m * (m - 1), 8 * m * (m + 1)), R("cm%d" % a, e, 64 * m, 4), F.Copy, accum=R("rs", m, m + 1))
+            elif m.isdigit():
+                m = int(m)
+                ts(R("cm%d" % LANE[m][0], LANE[m][1], 64 * m, 4), R("pr", 0, 16 * m), R("ow", 16 * m + 15, 16 * m + 16), A.is_lt)
+            elif m[0] == "a":
+                m = int(m[1:])
+                act(R("junk", 8 * m * (m - 1), 8 * m * (m + 1)), R("cm%d" % LANE[m][0], LANE[m][1], 64 * m, 4), F.Copy, accum=R("rs", m, m + 1))
             elif m[0] == "r":
-                m = int(m[1])
-                red(R("rs", m, m + 1), R("cm3", LANE[m][1], 64 * m, 4), A.add)
+                m = int(m[1:])
+                red(R("rs", m, m + 1), R("cm%d" % LANE[m][0], LANE[m][1], 64 * m, 4), A.add)
             else:
                 a = int(m[1])
                 quant(R("qc%d" % a), R("sc%d" % a), R("cm%d" % a))
                 mm(R("pr", 1024, 1024 + WD[a]), R("qg"), R("sg"), R("qc%d" % a), R("sc%d" % a), a == 1, a == 3)
-        if t == 0:
-            ts(R("dx"), R("jm"), col("p4m"), A.add, -300.0, A.max)
-            scan(R("mx"), R("z16"), R("mk"), A.min, A.max)
-            ts(R("dx", 15, 256, 16), R("dx", 15, 256, 16), 8192.0, A.add)
-            tail_constants()
-            plane(X, 1)
-        plane(X, 2)
-        plane(X, 3)
-        scan(R("exr"), pc, R("dx"), A.max, A.subtract)
-        tt(R("rt"), R("v1", 15, 256, 16), R("rs"), A.subtract)
-        tt(R("rk"), R("exr", 15, 256, 16), R("rt"), A.add)
-        ts(R("ro"), R("rk"), col("cro"), A.add)
         cp(R("win"), R("pay"), scatter=R("ro"))
-        scan(R("cum", 2, 514, 2), R("win"), R("c15"), A.add, A.add, 0.125)
-        all_ = R("cum", 512, 513)
-        count(1, all_)
-        scan(R("exw"), R("win"), R("mx"), A.add, A.mult)
-        tt(R("sq"), R("exw", 15, 256, 16), R("exw", 15, 256, 16), A.mult)
-        answer(1)
-        ts(R("ol"), R("sq"), 2.0 ** 82, A.mult, -2.0 ** 20, A.add)
-        ts(R("g1"), R("cum", 0, 512), 2.0 - 2.0 ** -8, A.mult, all_, A.add, off=col("id1"))
-        tt(R("key1"), R("ek"), R("kfr"), A.add, off=col("id1"))
-        red(col("bs1"), R("g1"), A.min)
-        xs = [lambda b=b: act(R("xs", PT * b, PT * b + 256), R("xp", 512 * b, 512 * b + 256), F.Copy, off=R("ol")) for b in range(4)]
-        count(2, col("bs1"))
-        xs[0]()
-        red(col("km1"), R("key1"), A.min)
-        tt(R("m1"), R("s2"), R("key1"), A.max)
-        ts(col("ex1"), col("id1"), col("kfo"), A.add, col("km1"), A.is_gt)
-        ts(R("f2"), R("s2"), col("km1"), A.add)
-        answer(2)
-        ts(R("ii", 0, 32, 2), R("m1"), col("km1"), A.is_gt)
-        ts(R("g2"), R("cum", 0, 512), 1.0 - 2.0 ** -9, A.mult, all_, A.add, off=col("id2"))
-        tt(R("key2"), R("ek"), R("kfr"), A.add, off=col("id2"))
-        red(col("bs2"), R("g2"), A.min)
-        count(3, col("bs2"))
-        for b in (1, 2, 3):
-            xs[b]()
-        red(col("km2"), R("key2"), A.min)
-        tt(R("m2"), R("f2"), R("key2"), A.max)
-        ts(col("ex2"), col("id2"), col("kfo"), A.add, col("km2"), A.is_gt)
-        ts(R("ff", 1, 32, 2), R("f2"), U9, A.mult)
-        answer(3)
-        ts(R("gg", 1, 32, 2), R("s2"), col("km2"), A.add, U9, A.mult)
-        tt(R("key3"), R("ek3"), R("kfr9"), A.add, off=col("id3"))
-        tt(R("kn3"), R("ek3n"), R("kfr9"), A.add, off=col("id3"))
-        red(col("km3"), R("key3"), A.min)
-        tt(R("m3"), R("gg", 1, 32, 2), R("key3"), A.max)
-        ts(R("ii", 1, 32, 2), R("m2"), col("km2"), A.is_gt)
-        ts(R("hh", 0, 32, 2), R("kn3"), col("km3"), A.is_le, col("km3"), A.add)
-        ts(R("hh", 1, 32, 2), R("m3"), col("km3"), A.is_gt)
-        tt(R("qq", 1, 64, 2), R("ii"), R("ff"), A.add)
-        tt(R("qq", 0, 64, 2), R("hh"), R("gg"), A.add)
-        scan(R("qo"), R("d4"), R("qq"), A.max, A.min)
-        ts(R("pl"), R("qo", 3, 64, 4), 256.0, A.mult)
+        h1, h3 = SPAN[0][1], SPAN[2][1]
+        scan(R("cum", 2, 2 * h1 + 2, 2), R("win", 0, h1), R("c3", 0, h1), A.add, A.add, 0.375 * ONE)
+        calls = {
+            "cum": lambda: scan(R("cum", 2 * h1 + 2, 2 * h3 + 2, 2), R("win", h1, h3), R("c3", h1, h3), A.add, A.add, R("cum", 2 * h1, 2 * h1 + 1)),
+            "c1": lambda: count(1, col("all")), "c2": lambda: count(2, col("bs1")), "c3": lambda: count(3, col("bs2")),
+            "id1": lambda: answer(1), "id2": lambda: answer(2), "id3": lambda: answer(3),
+            "exw": lambda: scan(R("exw"), R("win"), R("mx"), A.add, A.mult),
+            "sq": lambda: tt(R("sq"), R("exw", 15, 256, 16), R("exw", 15, 256, 16), A.mult),
+            "ol": lambda: ts(R("ol"), R("sq"), 2.0 ** 38, A.mult, -2.0 ** 20, A.add),
+            "x0": lambda: placed(0), "x1": lambda: placed(1), "x2": lambda: placed(2), "x3": lambda: placed(3),
+            "g1": lambda: ts(R("g1"), R("cum", 0, 2 * h1 + 2), 2.0, A.mult, col("all"), A.add, off=col("id1")),
+            "g2": lambda: ts(R("g2"), R("cum", 0, CW), 1.0, A.mult, col("all"), A.add, off=col("id2")),
+            "bs1": lambda: red(col("bs1"), R("g1"), A.min), "bs2": lambda: red(col("bs2"), R("g2"), A.min),
+            "key1": lambda: tt(R("key1"), R("ek"), R("kfr"), A.add, off=col("id1")),
+            "key2": lambda: tt(R("key2"), R("ek"), R("kfr"), A.add, off=col("id2")),
+            "key3": lambda: tt(R("key3"), R("ek3"), R("kfr"), A.add, off=col("id3")),
+            "kn3": lambda: tt(R("kn3"), R("ek3n"), R("kfr"), A.add, off=col("id3")),
+            "km1": lambda: red(col("km1"), R("key1"), A.min), "km2": lambda: red(col("km2"), R("key2"), A.min),
+            "km3": lambda: red(col("km3"), R("key3"), A.min),
+            "ex1": lambda: ts(col("ex1"), col("id1"), col("kfo"), A.add, col("km1"), A.is_gt),
+            "ex2": lambda: ts(col("ex2"), col("id2"), col("kfo"), A.add, col("km2"), A.is_gt),
+            "m1": lambda: tt(R("m1"), s2, R("key1"), A.max),
+            "m2": lambda: tt(R("m2"), R("ff", 1, 32, 2), R("key2"), A.max),
+            "m3": lambda: tt(R("m3"), R("qb", 0, 96, 6), R("key3"), A.max),
+            "ff": lambda: ts(R("ff", 1, 32, 2), s2, col("km1"), A.add),
+            "gg1": lambda: ts(R("qb", 0, 96, 6), s2, col("km2"), A.add),
+            "gg0": lambda: ts(R("qb", 4, 96, 6), s2, col("km3"), A.add),
+            "ii0": lambda: ts(R("ii", 0, 32, 2), R("m1"), col("km1"), A.is_gt, 512.0, A.mult),
+            "ii1": lambda: ts(R("ii", 1, 32, 2), R("m2"), col("km2"), A.is_gt, 512.0, A.mult),
+            "hh0": lambda: ts(R("qa", 4, 96, 6), R("kn3"), col("km3"), A.is_le, -512.0, A.mult),
+            "hh2": lambda: ts(R("qa", 5, 96, 6), R("kn3"), col("km3"), A.is_le, 512.0, A.mult),
+            "hh1": lambda: ts(R("qa", 1, 96, 6), R("m3"), col("km3"), A.is_gt, 512.0, A.mult),
+            "y1": lambda: tt(R("qb", 2, 96, 6), R("ii", 0, 32, 2), s2, A.add),
+            "y2": lambda: tt(R("qb", 3, 96, 6), R("ii", 1, 32, 2), R("ff", 1, 32, 2), A.add),
+            "min": lambda: scan(R("qo"), R("qa"), R("qb"), A.add, A.min),
+            "pl": lambda: ts(R("pl"), R("qo", 5, 96, 6), 0.5, A.mult),
+        }
+        for k in CUTS.split():
+            calls[k]()
         for o, lo, q, s, at in (("b13", 0, "qb%d" % t, "sb%d" % t, 0), ("b02", 8, "wbc%d" % t, "wbs%d" % t, 64)):
             for b in (0, 2, 1, 3):
                 pick("v" if b < 2 else "s", R(o, b, 512, 4), R("xs", PT * b, PT * b + PT), R("pl", lo, lo + 8))
@@ -505,36 +530,42 @@ def rank_program(g, core, T, topo):
         d2 = T.cores[(rank + 2) % N]
         send_one("b", "c", "wbc%d" % t, 128, d2, 0, t)
         send_one("b", "s", "wbs%d" % t, 128, d2, 0, t)
+        if t == 0:
+            last_iotas()
+            late_constants()
         for b in range(4):
             for k in range(2):
                 act(R("e2x", 128 * b + 64 * k, 128 * b + 64 * k + 64), R("xs", PT * b, PT * b + 64), F.Copy, scale=0.5)
-        if t == 0:
-            act(R("eh"), R("ex"), F.Copy, scale=0.5)
-            late_constants()
-        lands("adb%d" % t, 16, [R("wbc%d" % t, 0, 64), R("wbs%d" % t, 0, 64)])
-        lands("aob%d" % t, 32, [R("lbc%d" % t), R("lbs%d" % t)])
-        unpack("pr", "e", "wbc%d" % t, "wbs%d" % t, 0)
-        mix("pr", "za")
-        unpack("pd", "e", "lbc%d" % t, "lbs%d" % t, 0)
-        mix("pd", "zb")
-        layer("pr", "zb")
-        layer("pd", "za")
-        scaled("pr", "hb", "qh%d" % t, "sh%d" % t)
-        send_two("h", "c", "qh%d" % t, t)
-        send_two("h", "s", "sh%d" % t, t)
-        scaled("pd", "ha", "whc%d" % t, "whs%d" % t)
-        p2 = T.cores[(rank - 2) % N]
-        send_one("h", "c", "whc%d" % t, 0, p2, 128, t)
-        send_one("h", "s", "whs%d" % t, 0, p2, 128, t)
-        if t == 0:
-            later_constants()
-        ts(R("ft"), R("pl", 0, 16, 4), col("pfm"), A.subtract)
+        ts(R("ft"), R("pl", 0, 16, 4), col("pf1"), A.add)
         ts(R("r1"), R("ro"), 1.0, A.add)
-        tt(R("ft2"), R("ft"), R("fr4"), A.subtract)
+        tt(R("ft2"), R("ft"), R("fr8"), A.subtract)
         for c in range(4):
             ts(R("uu", c, 64, 4), R("r1"), R("ft2", c, c + 1), A.is_ge, R("ft2", c, c + 1), A.mult)
         scan(R("uo"), R("z4"), R("uu"), A.min, A.max)
         tt(R("w"), R("r1"), R("uo", 3, 64, 4), A.subtract)
+        before("v", (), [R("e2x")], "v")
+        lands("adb%d" % t, 16, [R("wbc%d" % t, 0, 64), R("wbs%d" % t, 0, 64)])
+        lands("aob%d" % t, 32, [R("lbc%d" % t), R("lbs%d" % t)])
+        for k in STEPS[t].split():
+            pb, z, src = ("pr", "za", "wb") if k[1] == "a" else ("pd", "zb", "lb")
+            for b in [int(c) for c in k[2:]]:
+                if k[0] == "U":
+                    unpack(pb, "e", src + "c%d" % t, src + "s%d" % t, 0, b)
+                elif k[0] == "M":
+                    tt(R(z, b, 512, 4), bank(pb, b), R("e2x", 128 * b, 128 * b + 128), A.add)
+                else:
+                    mm(bank(pb, b), R("wq", 128 * b, 128 * b + 128), R("wsc", 128 * b, 128 * b + 128), R("q" + z), R("s" + z))
+            if k[0] == "Q":
+                quant(R("q" + z), R("s" + z), R(z))
+            elif k == "Ha":
+                scaled(pb, "ha", "whc%d" % t, "whs%d" % t)
+            elif k == "Hb":
+                scaled(pb, "hb", "qh%d" % t, "sh%d" % t)
+                send_two("h", "c", "qh%d" % t, t)
+                send_two("h", "s", "sh%d" % t, t)
+        p2 = T.cores[(rank - 2) % N]
+        send_one("h", "c", "whc%d" % t, 0, p2, 128, t)
+        send_one("h", "s", "whs%d" % t, 0, p2, 128, t)
         cp(R("ri"), R("w"))
         ts(R("sb"), R("w"), 512.0, A.mult)
         ts(R("st"), R("w"), 64.0, A.is_ge, -4096.0, A.mult)
@@ -543,28 +574,33 @@ def rank_program(g, core, T, topo):
         tt(R("sa"), R("sa"), R("sb"), A.add)
         tt(R("sa"), R("sa"), R("cj"), A.max)
         cp(R("so"), R("sa"))
-        if t == 1:
+        if t == 0:
+            later_constants()
+        else:
             act(R("slr"), R("tb"), F.Copy, off=R("so"))
             dma("y", T.sl[:], T.slr[0:128:16, :], (), [R("slr")])
         lands("adh%d" % t, 16, [R("whc%d" % t, 128, 192), R("whs%d" % t, 128, 192)])
         lands("aoh%d" % t, 32, [R("lhc%d" % t), R("lhs%d" % t)])
-        unpack("pr", "f", "whc%d" % t, "whs%d" % t, 64)
-        renew("pr", "b02", 384)
-        unpack("pd", "f", "lhc%d" % t, "lhs%d" % t, 0)
-        renew("pd", "b13", 256)
+        for k in BACK.split():
+            b = int(k[1])
+            pb, src, at, old, to = ("pr", "wh", 64, "b02", 384) if k[0] == "a" else ("pd", "lh", 0, "b13", 256)
+            unpack(pb, "f", src + "c%d" % t, src + "s%d" % t, at, b)
+            tt(R("xp", 512 * b + to, 512 * b + to + 128), bank(pb, b), R(old, b, 512, 4), A.add)
         X2 = "xi%d" % (t + 1)
-        for q, b, lo, hi in (("s", 0, 0, 16), ("s", 1, 0, 16), ("v", 3, 0, 16), ("s", 2, 0, 8), ("v", 2, 8, 16)):
-            pick(q, R(X2, b + 64 * lo, 64 * hi, 4), R("xp", 512 * b, 512 * b + 512), R("so", lo, hi))
-        if t == 0:
-            quant(R("qx1"), R("sx1"), R(X2))
-    for h in range(2):
-        a, b = 128 * h, 128 * h + 128
-        quant(R("qx2", a, b), R("sx2", a, b), R("xi2", 4 * a, 4 * b))
-        mm(bank("pr", h), R("qv"), R("sv"), R("qx2", a, b), R("sx2", a, b))
+        for q, b, lo, hi in PICKS:
+            if q != "q":
+                pick(q, R(X2, b + 64 * lo, 64 * hi, 4), R("xp", 512 * b, 512 * b + 512), R("so", lo, hi))
+                continue
+            qn, sn = R("qx%d" % (t + 1), 16 * lo, 16 * hi), R("sx%d" % (t + 1), 16 * lo, 16 * hi)
+            quant(qn, sn, R(X2, 64 * lo, 64 * hi))
+            if t == 1:
+                mm(bank("pr", b), R("qv"), R("sv"), qn, sn)
+            elif b == 1:
+                mm(bank("pd", 0), R("qu2", 0, 128), R("su2", 0, 128), qn, sn)
     dma("y", T.oc[:], ap(R("qx2")).bitcast(dt.uint8), (), [R("qx2")])
     for k in range(4):
         dma("s" if k % 2 else "y", T.osc[4 * k:4 * k + 4, :], T.sx2[32 * k:32 * k + 4, :], (), [R("sx2")])
-    for h in range(2):
+    for h in (1, 0):
         cp(R("ycp", 128 * h, 128 * h + 128), bank("pr", h))
     dma("s", T.y[:], ap(R("ycp")), (), [R("ycp")])
     tot["loc"] = nloc[0]

from concourse.bass import DstId, RemoteDMATransfer
from concourse.mybir import dt, AluOpType as A, AxisListType, ActivationFunctionType as F

N = 8
C = 256
PT = 320
WD = (240, 256, 128, 128)
LANE = {15: (0, 0), 14: (0, 1), 13: (0, 2), 12: (0, 3), "in": (1, 0), 11: (1, 1), 10: (1, 2), 9: (1, 3)}
LANE.update({m: (2 + (8 - m) // 4, (8 - m) % 4) for m in range(1, 9)})
SHARE = (15, 14, 13)
ORDER = ("lo 12 lo2 sgn qg 11 10 9 a12 8 in a11 a10 6 7 mf a9 5 v1 q1 a7 1 q2 a8 2 3 4 a6 q0 q3 r1 r5 r3 rk r2 r4 rt pay exr tc all p0 p1 p2 p3 ro",
         "lo 12 lo2 10 11 in 9 a9 8 a10 a12 a11 q1 7 6 a6 5 a7 2 3 v1 4 q2 1 a8 q0 q3 rk r4 sgn r3 r5 r1 r2 all rt exr pay p2 p3 ro")
CUTS = ("c1 exw cum id1 g1 key1 bs1 c2 sq km1 m1 ol ex1 x0 ff id2 ii0 g2 key2 bs2 c3 km2 m2 ex2 gg1 x1 x2 x3 ii1 id3 y1 key3 kn3 km3 m3 y2 "
        "gg0 hh0 hh2 hh1 min pl")
STEPS = ("Ua0123 Ma0123 Qa Ub0123 Wa20 Mb0123 Qb Wb2031 Wa31 Hb Ha", "Ua01 Ma01 Ub0123 Mb0123 Ua23 Qb Wb2031 Ma23 Qa Wa2031 Hb Ha")
BACK = "a0 a1 a2 a3 b0 b1 b2 b3"
PICKS = (("s", 0, 0, 16), ("s", 1, 0, 16), ("v", 2, 8, 16), ("v", 3, 0, 16), ("s", 2, 0, 8), ("q", 1, 8, 16), ("q", 0, 0, 8))
ONE = 2 ** 21
SCRATCH = {}
PLACE = {}
PSUM = ("pr", "pd")


def _spans():
    lo, hi, out = 0, 0, []
    for m in (4, 3, 2):
        lo, hi = lo - (-(C - lo) // (2 * m - 1)), hi - (-2 * (C - hi) // (m + 1))
        out.append((lo, hi))
    return out


SPAN = _spans()
E3, EK = 2 * SPAN[2][0], 2 * SPAN[2][1] + 2
CW = 2 * SPAN[1][1] + 2


def _decl():
    f, b, i, h, q, s = "float32", "bfloat16", "int32", "uint16", "float8_e4m3fn_x4", "uint8"

    def add(names, n, d, where="sbuf"):
        for k in names.split():
            SCRATCH[k] = (where, [128, n], d)
            PLACE[k] = (k, 0, n)

    def share(buf, d, *groups):
        at = 0
        for names, n in groups:
            for k in names.split():
                PLACE[k] = (buf, at, n)
                at += -(-n // 32) * 32
        SCRATCH[buf] = ("sbuf", [128, at], d)
    add("pr pd", 2048, f, "psum")
    add("ub vb", 512, b)
    add("qu qv", 128, q), add("su sv", 128, s)
    add("qu2", 256, q), add("su2", 256, s)
    add("wq", 512, q), add("wsc", 512, s)
    share("ci", i, ("iP pq pb2 pb3 pg", 2))
    share("cfl", f, ("jm ab mk d0 z16 mx kc c3", 256), ("ek", EK), ("ek3 ek3n", EK - E3 + 8), ("tb", 512),
          ("pf k1 kf kfo gpf p4 pf1 pfm p4m cro c0", 2), ("iL", 8), ("c16 kq kfr s1 cj d15", 16), ("fr4 fr8", 4), ("z4", 64))
    add("ul", 16, h)
    add("gt", 512, b), add("iC", 128, b), add("hf ex eh", 516, b), add("dv", 256, b)
    share("qk", q, ("qg qe0 qe1 qe2 qe3 qf0 qf1 qf2 qf3", 128)), share("sk", s, ("sg se0 se1 se2 se3 sf0 sf1 sf2 sf3", 128))
    for k in range(4):
        add("cm%d" % k, 4 * WD[k], b)
    share("qc", q, *[("qc%d" % k, WD[k]) for k in range(4)]), share("sc", s, *[("sc%d" % k, WD[k]) for k in range(4)])
    add("dx dd ow sgn pay exr win exw ycp slr", 256, f), add("cum", 520, f), add("v1", 256, b)
    add("junk", 1920, b), add("junk2", 384, b), add("rl13 rl14 rl15", 256, b)
    share("sm", f, ("rs rk sq g1 g2 key1 key2 key3 kn3 m1 m2 m3 r1 w sa sb st", 16), ("ii ff", 32), ("uu uo", 64), ("qa qb qo", 96),
          ("ac1 ac2 ac3 bs1 bs2 km1 km2 km3 ex1 ex2 sgs all", 2), ("ft ft2", 4))
    share("li", h, ("ro pl so ol ri", 16), ("id1 id2 id3", 2))
    add("xp", 2048, b), add("xs", 4 * PT, b), add("e2x", 512, b)
    add("b13 b02 za zb ha hb", 512, b), add("qza qzb", 128, q), add("sza szb", 128, s)
    for t in range(3):
        add("xi%d" % t, 1024, b), add("qx%d" % t, 256, q), add("sx%d" % t, 256, s)
    for t in range(2):
        add("qb%d lbc%d lhc%d qh%d" % ((t,) * 4), 128, q)
        add("sb%d lbs%d lhs%d sh%d" % ((t,) * 4), 128, s)
        add("wbc%d whc%d" % (t, t), 192, q), add("wbs%d whs%d" % (t, t), 192, s)
        add("rbc%d rhc%d" % (t, t), 64, q), add("rbs%d rhs%d" % (t, t), 64, s)


_decl()
SEMAPHORES = ["ev", "es", "et", "eg", "loc"] + ["d%d" % k for k in range(21)] + [
    "%s%s%d" % (a, b, t) for a in ("rc", "rs", "ao", "ad") for b in "bh" for t in range(2)]


def _relays(topo, cores, r):
    c = cores[r]
    own = [d for d in topo.cores_of(c) if d != c and topo.may_write(d, cores[(r + 1) % N]) and topo.may_write(d, cores[(r + 3) % N])]
    near, far = [[d for d in own if (topo.die(d) == topo.die(c)) == same] for same in (True, False)]
    return [(near[0], "c", 0), (near[-1], "s", 0), (far[0], "c", 1), (far[-1], "s", 1)]


def _mask(engines):
    return sum(1 << int(e) for e in engines)


def _relay(g, core, T, topo, r, w, i):
    n = 0
    for t in range(2):
        for ph in "bh":
            k = 2 * i + 1
            dst = T.cores[(r + (k if ph == "b" else -k)) % N]
            rid, pid = topo.addr(dst, core)
            en = topo.engines(core, dst)
            g.wait_ge(T.sem["r%s%s%d" % (w, ph, t)], 8)
            src, d = T["r%s%s%d" % (ph, w, t)][:, 0:64], T["l%s%s%d" % (ph, w, t)][:, 64 * i:64 * i + 64]
            if w == "c":
                src, d = src.bitcast(dt.uint8), d.bitcast(dt.uint8)
            g.remote_dma(out_ap=d, in_ap=src, remote_sem=T.sem["ao%s%d" % (ph, t)], local_sem=T.sem.loc, pid=pid, routing_id=rid,
                         dma_engine_mask=_mask(en))
            n += len(en)
    g.wait_ge(T.sem.loc, n)


def rank_program(g, core, T, topo):
    rank = T.rank_of(core)
    if rank is None:
        for r in range(N):
            if core in topo.cores_of(T.cores[r]):
                for d, w, i in _relays(topo, T.cores, r):
                    if d == core:
                        _relay(g, core, T, topo, r, w, i)
        return
    eng = {"v": g.vector, "s": g.scalar, "t": g.tensor, "g": g, "y": g.sync}
    seen = {q: {} for q in eng}
    tot, snap, acc, nd = {}, {}, {}, [0]

    def R(n, lo=0, hi=None, st=1):
        buf, at, w = PLACE[n]
        return (buf, at + lo, at + (w if hi is None else hi), st)

    def ap(r):
        n, lo, hi, st = r
        return T[n][:, lo:hi] if st == 1 else T[n][:, lo:hi:st]

    def meet(a, b):
        if a[0] in PSUM:
            return a[1] // 512 <= (b[2] - 1) // 512 and b[1] // 512 <= (a[2] - 1) // 512
        if a[1] >= b[2] or b[1] >= a[2]:
            return False
        return not (a[3] == b[3] and a[3] > 1 and (a[1] - b[1]) % a[3])

    def wait(q, sem, val):
        if seen[q].get(sem, 0) >= val:
            return
        eng[q].wait_ge(T.sem[sem], val)
        seen[q][sem] = val
        for k, v in snap.get((sem, val), {}).items():
            seen[q][k] = max(seen[q].get(k, 0), v)

    def before(q, outs, ins, own, open_=False):
        need = {}
        for r, wr in [(r, True) for r in outs] + [(r, False) for r in ins]:
            for o, ow, sem, val, oq in acc.get(r[0], ()):
                if not (wr or ow or (r[0] in PSUM and oq != own)) or not meet(r, o):
                    continue
                if oq == own == "t" and open_:
                    continue
                need[sem] = max(need.get(sem, 0), val)
        for sem in sorted(need):
            wait(q, sem, need[sem])

    def after(q, outs, ins, sem, val, own):
        snap[(sem, val)] = dict(seen[q])
        for r in outs:
            l = acc.setdefault(r[0], [])
            if r[3] == 1 and r[0] not in PSUM:
                l[:] = [e for e in l if not (e[0][1] >= r[1] and e[0][2] <= r[2])]
            l.append((r, True, sem, val, own))
        for r in ins:
            acc.setdefault(r[0], []).append((r, False, sem, val, own))

    def op(q, outs, ins, call, open_=False):
        before(q, outs, ins, q, open_)
        sem = "e" + q
        tot[sem] = tot.get(sem, 0) + 1
        call(eng[q]).then_inc(T.sem[sem], 1)
        after(q, outs, ins, sem, tot[sem], q)

    def dma(q, out, in_, outs=(), ins=()):
        before(q, outs, ins, "dma")
        sem = "d%d" % nd[0]
        nd[0] += 1
        tot[sem] = 16
        eng[q].dma_start(out, in_).then_inc(T.sem[sem], 16)
        after(q, outs, ins, sem, 16, "dma")

    def lands(sem, val, regions):
        tot[sem] = val
        after("g", regions, (), sem, val, "remote")
        snap[(sem, val)] = {}

    def ts(out, i, s1, op0, s2=None, op1=None, off=None):
        cols = [s for s in (s1, s2) if isinstance(s, tuple)]
        a1 = ap(s1) if isinstance(s1, tuple) else s1
        a2 = ap(s2) if isinstance(s2, tuple) else s2
        src = ap(i) if off is None else ap(i).indirect(ap(off))
        kw = {} if op1 is None else {"op1": op1}
        op("v", [out], [i] + cols + ([off] if off else []),
           lambda e: e.tensor_scalar(out=ap(out), in0=src, scalar1=a1, scalar2=a2, op0=op0, **kw))

    def tt(out, a, b, o, off=None):
        src = ap(a) if off is None else ap(a).indirect(ap(off))
        op("v", [out], [a, b] + ([off] if off else []), lambda e: e.tensor_tensor(out=ap(out), in0=src, in1=ap(b), op=o))

    def cp(out, i, off=None, scatter=None):
        src = ap(i) if off is None else ap(i).indirect(ap(off))
        dst = ap(out) if scatter is None else ap(out).indirect(ap(scatter))
        op("v", [out], [i] + [o for o in (off, scatter) if o], lambda e: e.tensor_copy(out=dst, in_=src))

    def scan(out, a, b, o0, o1, first=0.0):
        at = isinstance(first, tuple)
        op("v", [out], [a, b] + [first] * at,
           lambda e: e.tensor_tensor_scan(out=ap(out), data0=ap(a), data1=ap(b), initial=ap(first) if at else first, op0=o0, op1=o1))

    def red(out, i, o):
        op("v", [out], [i], lambda e: e.tensor_reduce(out=ap(out), in_=ap(i), axis=AxisListType.X, op=o))

    def fill(out, c):
        op("v", [out], [], lambda e: e.memset(ap(out), c))

    def act(out, i, fn, bias=None, scale=None, accum=None, off=None):
        src = ap(i) if off is None else ap(i).indirect(ap(off))
        kw = {}
        if bias is not None:
            kw["bias"] = ap(bias) if isinstance(bias, tuple) else bias
        if scale is not None:
            kw["scale"] = scale
        if accum is not None:
            kw["accum_out"] = ap(accum)
        op("s", [out] + ([accum] if accum else []), [i] + [o for o in (bias, off) if isinstance(o, tuple)],
           lambda e: e.activation(out=ap(out), in_=src, func=fn, **kw))

    def pick(q, out, i, off):
        if q == "v":
            cp(out, i, off=off)
        else:
            act(out, i, F.Copy, off=off)

    def quant(q, s, i):
        op("v", [q, s], [i], lambda e: e.quantize_mx(ap(q), ap(s), ap(i)))

    def mm(out, l, ls, r, rs, start=True, stop=True):
        op("t", [out], [l, ls, r, rs], lambda e: e.matmul_mx(ap(out), ap(l), ap(ls), ap(r), ap(rs), start, stop), not start)

    def iota(out, pattern, base, cm, flag=True):
        kw = {"allow_small_or_imprecise_dtypes": True} if flag else {}
        op("g", [out], [], lambda e: e.iota(ap(out), pattern, base, cm, **kw))

    def select(out, i, pattern, cmp, c, base, cm):
        op("g", [out], [i], lambda e: e.affine_select(ap(out), ap(i), pattern, cmp, c, base, cm))

    def col(n):
        return R(n, 0, 1)

    def plane(x, b):
        act(R("xp", 512 * b, 512 * b + 256), R(x, b, 1024, 4), F.Copy)

    def nought(m):
        a, e = LANE[m]
        iota(R("cm%d" % a, 64 * m + e, 4 * WD[a], 4), [[0, WD[a] - 16 * m]], 0, 0)

    dma("y", ap(R("ub")), T.u[:], [R("ub")])
    dma("y", ap(R("xi0")), T.x[:], [R("xi0")])
    fill(R("cm3", 64), 0.0)
    fill(R("dv"), -64.0)
    iota(R("iP"), [[0, 2]], 0, 1, False)
    iota(R("iL"), [[16, 8]], 0, 0)
    iota(R("jm"), [[0, 16], [-4096, 16]], 0, 0)
    iota(R("iC"), [[1, 8], [0, 16]], 0, 0)
    iota(R("z16"), [[0, 256]], 1, 0)
    iota(R("z16", 0, 256, 16), [[0, 16]], 0, 0)
    for m in (9, 10, 11):
        nought(m)
    iota(R("dv", 0, 256, 16), [[16, 16]], 15, 0)
    for m in (12, 13, 14):
        nought(m)
    iota(R("kc"), [[1, 256]], ONE, 0)
    iota(R("c16"), [[16, 16]], 15, 0)
    iota(R("rs", 0, 1), [[0, 1]], 0, 0)
    iota(R("kq"), [[-1, 2], [2, 2], [0, 4]], 1, 0)
    iota(R("s1"), [[0, 4], [32, 4]], 0, 0)
    iota(R("c3"), [[0, 256]], 3 * ONE, 0)
    iota(R("ek", 8), [[1, EK - 8]], 8, 0)
    iota(R("ek", 0, 8), [[0, 8]], 4096, 0)
    iota(R("qa"), [[0, 96]], 0, 0)
    iota(R("qa", 0, 96, 6), [[0, 16]], 4096, 0)
    iota(R("qb"), [[0, 96]], 4096, 0)
    iota(R("ek3", 0, 8), [[0, 8]], 4096, 0)
    iota(R("ek3n", 0, 8), [[0, 8]], -1, 0)

    def more_iotas():
        iota(R("hf"), [[0, 516]], 1, 0)
        select(R("ex"), R("hf"), [[-1, 516]], A.is_equal, 0.0, 3, 4)
        iota(R("fr4"), [[1, 4]], 0, 0)
        iota(R("z4"), [[0, 16], [4096, 4]], 0, 0)

    def last_iotas():
        iota(R("tb", 0, 256), [[0, 256]], -1, 0)
        iota(R("tb", 256, 384), [[128, 2], [1, 64]], 64, 0)
        iota(R("tb", 384, 512), [[128, 2], [1, 64]], 0, 0)
    ts(R("pq"), R("iP"), 15, A.bitwise_and)
    ts(R("pb2"), R("iP"), 2, A.arith_shift_right, 1, A.bitwise_and)
    ts(R("pb3"), R("iP"), 3, A.arith_shift_right, 1, A.bitwise_and)
    ts(R("pg"), R("iP"), 4, A.arith_shift_right)
    ts(R("pf"), R("pq"), -1.0, A.mult)
    ts(R("k1"), R("pb2"), 2.0, A.mult, 1.0, A.add)
    cp(R("gpf"), R("pg"))
    tt(R("kf"), R("k1"), R("pb3"), A.subtract)
    ts(R("ul", 0, 8), R("iL"), 4.0, A.add)
    ts(R("ul", 8, 16), R("iL"), col("kf"), A.add)
    act(R("p4"), R("pf"), F.Copy, scale=-4096.0)
    act(R("ab"), R("jm"), F.Abs, bias=col("p4"))
    act(R("mk"), R("ab"), F.Identity, bias=2.0 ** 91, scale=-2.0 ** 80)
    quant(R("qu"), R("su"), R("ub"))
    op("v", [R("qu2")], [R("qu"), R("ul")],
       lambda e: e.tensor_copy(ap(R("qu2")).bitcast(dt.uint32), ap(R("qu")).bitcast(dt.uint32).indirect(ap(R("ul")))))
    act(R("su2"), R("su"), F.Copy, off=R("ul"))
    act(R("d0"), R("jm"), F.Identity, bias=-2.0 ** 91, scale=-2.0 ** 80)
    quant(R("qx0"), R("sx0"), R("xi0"))
    for e in range(4):
        ts(R("gt", e, 512, 4), R("iC"), col("gpf"), A.is_equal)
    scan(R("mx"), R("z16"), R("mk"), A.min, A.max)
    before("y", (), [R("xi0")], "dma")
    for to in [R("cm2", 320)] + [R("xs", PT * b + 256, PT * b + PT) for b in range(4)]:
        zero = R("cm3", 256, 256 + to[2] - to[1])
        dma("y", ap(to), ap(zero), [to], [zero])
    dma("y", ap(R("cum", 4, CW)), ap(R("jm", 0, CW - 4)), [R("cum", 4, CW)], [R("jm", 0, CW - 4)])
    dma("y", ap(R("wq")).bitcast(dt.uint8), T.wc[:], [R("wq")])
    dma("y", ap(R("wsc")), T.ws[:], [R("wsc")])
    dma("y", ap(R("vb")), T.v[:], [R("vb")])
    for k in ("ek3", "ek3n"):
        dma("y", ap(R(k, 8)), ap(R("ek", E3, EK)), [R(k, 8)], [R("ek", E3, EK)])
    s2 = R("ff", 0, 32, 2)

    def tail_constants():
        act(R("cum", 0, 4), R("c16", 0, 4), F.Identity, bias=4096.0 * ONE, scale=0.0)
        act(R("pfm"), R("pf"), F.Identity, bias=0.5, scale=-2.0)
        act(R("kfr"), R("kq"), F.Copy, scale=0.0625)
        act(R("kfo"), R("kf"), F.Copy, scale=0.0625)
        act(s2, R("s1"), F.Identity, bias=col("pfm"))

    def late_constants():
        act(R("eh"), R("ex"), F.Copy, scale=0.5)
        act(R("pf1"), R("pf"), F.Identity, bias=1.0)
        act(R("fr8"), R("fr4"), F.Copy, scale=0.125)
        ts(R("cj"), R("c16"), col("pf"), A.subtract, -15.0, A.add)
        for b in range(4):
            quant(R("qe%d" % b), R("se%d" % b), R("eh", 3 - b, 515 - b))

    def later_constants():
        for b in range(4):
            quant(R("qf%d" % b), R("sf%d" % b), R("ex", 3 - b, 515 - b))
        quant(R("qv"), R("sv"), R("vb"))

    rel = {(w, i): d for d, w, i in _relays(topo, T.cores, rank)}
    nloc = [0]

    def view(n, a, b, w):
        v = T[n][:, a:b]
        return v.bitcast(dt.uint8) if w == "c" else v

    def send_two(ph, w, src, t):
        before("g", (), [R(src)], "remote")
        tr = []
        for i in range(2):
            rid, pid = topo.addr(rel[(w, i)], core)
            en = topo.engines(core, rel[(w, i)])
            h = len(en) // 2
            en = en[i * h:i * h + h]
            tr.append(RemoteDMATransfer(dst_ids=[DstId(rid=rid, pnc=pid)], dma_engine_mask=_mask(en), remote_sem=T.sem["r%s%s%d" % (w, ph, t)],
                                        src=view(src, 64 * i, 64 * i + 64, w), dst=view("r%s%s%d" % (ph, w, t), 0, 64, w)))
            nloc[0] += h
        g.remote_dma_fused(tr, local_sem=T.sem.loc)

    def send_one(ph, w, src, a, dst, to, t):
        before("g", (), [R(src, a, a + 64)], "remote")
        rid, pid = topo.addr(dst, core)
        en = topo.engines(core, dst)
        g.remote_dma(out_ap=view(src, to, to + 64, w), in_ap=view(src, a, a + 64, w), remote_sem=T.sem["ad%s%d" % (ph, t)],
                     local_sem=T.sem.loc, pid=pid, routing_id=rid, dma_engine_mask=_mask(en))
        nloc[0] += len(en)

    def bank(ps, b):
        return R(ps, 512 * b, 512 * b + 128)

    def unpack(ps, e, q, s, off, b):
        mm(bank(ps, b), R("q%s%d" % (e, b)), R("s%s%d" % (e, b)), R(q, off, off + 128), R(s, off, off + 128))

    def scaled(ps, h, qh, sh):
        for b in (2, 0, 3, 1):
            if b < 2:
                ts(R(h, b, 512, 4), bank(ps, b), 0.03125, A.mult)
            else:
                act(R(h, b, 512, 4), bank(ps, b), F.Copy, scale=0.03125)
        quant(R(qh, 0, 128), R(sh, 0, 128), R(h))

    def count(n, bias):
        lo, hi = SPAN[n - 1]
        act(R("junk2", 128 * n - 128, 128 * n - 128 + hi - lo), R("cum", 2 * lo, 2 * hi, 2), F.Sign, bias=bias, scale=float(n - 5),
            accum=col("ac%d" % n))

    def answer(n):
        lo, hi = SPAN[n - 1]
        if n == 1:
            ts(col("id1"), col("ac1"), float(lo + hi), A.add)
        else:
            ts(col("id%d" % n), col("ac%d" % n), float(lo + hi - (E3 - 8 if n == 3 else 0)), A.add, col("ex%d" % (n - 1)), A.mult)

    def placed(b):
        act(R("xs", PT * b, PT * b + 256), R("xp", 512 * b, 512 * b + 256), F.Copy, off=R("ol"))

    for t in range(2):
        X, Q, S = "xi%d" % t, "qx%d" % t, "sx%d" % t
        pa, ps, pv, pc = R("pr", 0, 256), R("pr", 1536, 1792), R("pr", 512, 768), R("pr", 1024, 1280)
        mm(pa, R("qu2", 0, 128), R("su2", 0, 128), R(Q), R(S))
        mm(ps, R("qu2", 0, 128), R("su2", 0, 128), R(Q), R(S))
        mm(pv, R("qu2", 128, 256), R("su2", 128, 256), R(Q), R(S))
        if t == 0:
            act(R("p4m"), R("pf"), F.Identity, bias=-2048.0, scale=-4096.0)
            act(R("c0"), R("pf"), F.Square, bias=16.0)
            act(R("dx"), R("jm"), F.Identity, bias=col("p4m"))
            act(R("cro"), R("c0"), F.Identity, bias=col("pf"), scale=-2048.0)
            act(R("d15"), R("dx", 15, 256, 16), F.Identity, bias=2.0 ** 20)
            act(R("cro"), R("cro"), F.Identity, bias=2.0 ** 20)
        else:
            plane(X, 0)
            plane(X, 1)
        top = 128 if t else 192
        tt(R("dd", top, 256), bank("pd", 0) if t else R("pr", top, 256), R("mk", top, 256), A.min)
        scan(R("ow", top, 256), R("d0", top, 256), R("dd", top, 256), A.min, A.max)
        for m in SHARE:
            act(R("rl%d" % m, 0, 16 * m), R("pr", 1536, 1536 + 16 * m), F.Relu, bias=R("ow", 16 * m + 15, 16 * m + 16), scale=-1.0)
        for m in (SHARE[1], SHARE[0], SHARE[2]):
            act(R("cm%d" % LANE[m][0], LANE[m][1], 64 * m, 4), R("rl%d" % m, 0, 16 * m), F.Sign, accum=R("rs", m, m + 1))
        if t == 0:
            more_iotas()
        for m in ORDER[t].split():
            if m == "qg":
                quant(R("qg"), R("sg"), R("gt"))
            elif m == "mf":
                ts(R("mx", 15, 256, 16), R("mx", 15, 256, 16), 2.0 ** -121, A.mult)
            elif m == "sgn":
                act(R("sgn"), pv, F.Sign, bias=-2.0 ** -120, accum=col("sgs"))
            elif m == "all":
                act(col("all"), col("sgs"), F.Identity, bias=3.0 * C * ONE, scale=float(ONE))
            elif m == "tc":
                tail_constants()
            elif m in ("p0", "p1", "p2", "p3"):
                plane(X, int(m[1]))
            elif m == "exr":
                scan(R("exr"), pc, R("dx"), A.max, A.subtract)
            elif m == "rk":
                tt(R("rk"), R("d15"), R("v1", 15, 256, 16), A.subtract)
            elif m == "rt":
                tt(R("dx", 15, 256, 16), R("rk"), R("rs"), A.add)
            elif m == "ro":
                ts(R("ro"), R("exr", 15, 256, 16), col("cro"), A.add)
            elif m == "lo":
                tt(R("dd", 0, top), R("pr", 0, top), R("mk", 0, top), A.min)
            elif m == "lo2":
                scan(R("ow", 0, top), R("d0", 0, top), R("dd", 0, top), A.min, A.max)
            elif m == "in":
                tt(R("cm1", 0, 1024, 4), pa, R("ow"), A.is_le)
            elif m == "v1":
                scan(R("v1"), R("dv"), R("cm1", 0, 1024, 4), A.max, A.subtract, -64.0)
            elif m == "pay":
                scan(R("pay"), R("kc"), R("sgn"), A.max, A.mult)
            elif m.isdigit():
                m = int(m)
                ts(R("cm%d" % LANE[m][0], LANE[m][1], 64 * m, 4), R("pr", 0, 16 * m), R("ow", 16 * m + 15, 16 * m + 16), A.is_lt)
            elif m[0] == "a":
                m = int(m[1:])
                act(R("junk", 8 * m * (m - 1), 8 * m * (m + 1)), R("cm%d" % LANE[m][0], LANE[m][1], 64 * m, 4), F.Copy, accum=R("rs", m, m + 1))
            elif m[0] == "r":
                m = int(m[1:])
                red(R("rs", m, m + 1), R("cm%d" % LANE[m][0], LANE[m][1], 64 * m, 4), A.add)
            else:
                a = int(m[1])
                quant(R("qc%d" % a), R("sc%d" % a), R("cm%d" % a))
                mm(R("pr", 1024, 1024 + WD[a]), R("qg"), R("sg"), R("qc%d" % a), R("sc%d" % a), a == 1, a == 3)
        cp(R("win"), R("pay"), scatter=R("ro"))
        h1, h3 = SPAN[0][1], SPAN[2][1]
        scan(R("cum", 2, 2 * h1 + 2, 2), R("win", 0, h1), R("c3", 0, h1), A.add, A.add, 0.375 * ONE)
        calls = {
            "cum": lambda: scan(R("cum", 2 * h1 + 2, 2 * h3 + 2, 2), R("win", h1, h3), R("c3", h1, h3), A.add, A.add, R("cum", 2 * h1, 2 * h1 + 1)),
            "c1": lambda: count(1, col("all")), "c2": lambda: count(2, col("bs1")), "c3": lambda: count(3, col("bs2")),
            "id1": lambda: answer(1), "id2": lambda: answer(2), "id3": lambda: answer(3),
            "exw": lambda: scan(R("exw"), R("win"), R("mx"), A.add, A.mult),
            "sq": lambda: tt(R("sq"), R("exw", 15, 256, 16), R("exw", 15, 256, 16), A.mult),
            "ol": lambda: ts(R("ol"), R("sq"), 2.0 ** 38, A.mult, -2.0 ** 20, A.add),
            "x0": lambda: placed(0), "x1": lambda: placed(1), "x2": lambda: placed(2), "x3": lambda: placed(3),
            "g1": lambda: ts(R("g1"), R("cum", 0, 2 * h1 + 2), 2.0, A.mult, col("all"), A.add, off=col("id1")),
            "g2": lambda: ts(R("g2"), R("cum", 0, CW), 1.0, A.mult, col("all"), A.add, off=col("id2")),
            "bs1": lambda: red(col("bs1"), R("g1"), A.min), "bs2": lambda: red(col("bs2"), R("g2"), A.min),
            "key1": lambda: tt(R("key1"), R("ek"), R("kfr"), A.add, off=col("id1")),
            "key2": lambda: tt(R("key2"), R("ek"), R("kfr"), A.add, off=col("id2")),
            "key3": lambda: tt(R("key3"), R("ek3"), R("kfr"), A.add, off=col("id3")),
            "kn3": lambda: tt(R("kn3"), R("ek3n"), R("kfr"), A.add, off=col("id3")),
            "km1": lambda: red(col("km1"), R("key1"), A.min), "km2": lambda: red(col("km2"), R("key2"), A.min),
            "km3": lambda: red(col("km3"), R("key3"), A.min),
            "ex1": lambda: ts(col("ex1"), col("id1"), col("kfo"), A.add, col("km1"), A.is_gt),
            "ex2": lambda: ts(col("ex2"), col("id2"), col("kfo"), A.add, col("km2"), A.is_gt),
            "m1": lambda: tt(R("m1"), s2, R("key1"), A.max),
            "m2": lambda: tt(R("m2"), R("ff", 1, 32, 2), R("key2"), A.max),
            "m3": lambda: tt(R("m3"), R("qb", 0, 96, 6), R("key3"), A.max),
            "ff": lambda: ts(R("ff", 1, 32, 2), s2, col("km1"), A.add),
            "gg1": lambda: ts(R("qb", 0, 96, 6), s2, col("km2"), A.add),
            "gg0": lambda: ts(R("qb", 4, 96, 6), s2, col("km3"), A.add),
            "ii0": lambda: ts(R("ii", 0, 32, 2), R("m1"), col("km1"), A.is_gt, 512.0, A.mult),
            "ii1": lambda: ts(R("ii", 1, 32, 2), R("m2"), col("km2"), A.is_gt, 512.0, A.mult),
            "hh0": lambda: ts(R("qa", 4, 96, 6), R("kn3"), col("km3"), A.is_le, -512.0, A.mult),
            "hh2": lambda: ts(R("qa", 5, 96, 6), R("kn3"), col("km3"), A.is_le, 512.0, A.mult),
            "hh1": lambda: ts(R("qa", 1, 96, 6), R("m3"), col("km3"), A.is_gt, 512.0, A.mult),
            "y1": lambda: tt(R("qb", 2, 96, 6), R("ii", 0, 32, 2), s2, A.add),
            "y2": lambda: tt(R("qb", 3, 96, 6), R("ii", 1, 32, 2), R("ff", 1, 32, 2), A.add),
            "min": lambda: scan(R("qo"), R("qa"), R("qb"), A.add, A.min),
            "pl": lambda: ts(R("pl"), R("qo", 5, 96, 6), 0.5, A.mult),
        }
        for k in CUTS.split():
            calls[k]()
        for o, lo, q, s, at in (("b13", 0, "qb%d" % t, "sb%d" % t, 0), ("b02", 8, "wbc%d" % t, "wbs%d" % t, 64)):
            for b in (0, 2, 1, 3):
                pick("v" if b < 2 else "s", R(o, b, 512, 4), R("xs", PT * b, PT * b + PT), R("pl", lo, lo + 8))
            quant(R(q, at, at + 128), R(s, at, at + 128), R(o))
            if lo == 0:
                send_two("b", "c", q, t)
                send_two("b", "s", s, t)
        d2 = T.cores[(rank + 2) % N]
        send_one("b", "c", "wbc%d" % t, 128, d2, 0, t)
        send_one("b", "s", "wbs%d" % t, 128, d2, 0, t)
        if t == 0:
            last_iotas()
            late_constants()
        for b in range(4):
            for k in range(2):
                act(R("e2x", 128 * b + 64 * k, 128 * b + 64 * k + 64), R("xs", PT * b, PT * b + 64), F.Copy, scale=0.5)
        ts(R("ft"), R("pl", 0, 16, 4), col("pf1"), A.add)
        ts(R("r1"), R("ro"), 1.0, A.add)
        tt(R("ft2"), R("ft"), R("fr8"), A.subtract)
        for c in range(4):
            ts(R("uu", c, 64, 4), R("r1"), R("ft2", c, c + 1), A.is_ge, R("ft2", c, c + 1), A.mult)
        scan(R("uo"), R("z4"), R("uu"), A.min, A.max)
        tt(R("w"), R("r1"), R("uo", 3, 64, 4), A.subtract)
        before("v", (), [R("e2x")], "v")
        lands("adb%d" % t, 16, [R("wbc%d" % t, 0, 64), R("wbs%d" % t, 0, 64)])
        lands("aob%d" % t, 32, [R("lbc%d" % t), R("lbs%d" % t)])
        for k in STEPS[t].split():
            pb, z, src = ("pr", "za", "wb") if k[1] == "a" else ("pd", "zb", "lb")
            for b in [int(c) for c in k[2:]]:
                if k[0] == "U":
                    unpack(pb, "e", src + "c%d" % t, src + "s%d" % t, 0, b)
                elif k[0] == "M":
                    tt(R(z, b, 512, 4), bank(pb, b), R("e2x", 128 * b, 128 * b + 128), A.add)
                else:
                    mm(bank(pb, b), R("wq", 128 * b, 128 * b + 128), R("wsc", 128 * b, 128 * b + 128), R("q" + z), R("s" + z))
            if k[0] == "Q":
                quant(R("q" + z), R("s" + z), R(z))
            elif k == "Ha":
                scaled(pb, "ha", "whc%d" % t, "whs%d" % t)
            elif k == "Hb":
                scaled(pb, "hb", "qh%d" % t, "sh%d" % t)
                send_two("h", "c", "qh%d" % t, t)
                send_two("h", "s", "sh%d" % t, t)
        p2 = T.cores[(rank - 2) % N]
        send_one("h", "c", "whc%d" % t, 0, p2, 128, t)
        send_one("h", "s", "whs%d" % t, 0, p2, 128, t)
        cp(R("ri"), R("w"))
        ts(R("sb"), R("w"), 512.0, A.mult)
        ts(R("st"), R("w"), 64.0, A.is_ge, -4096.0, A.mult)
        ts(R("sa"), R("ri"), -511.0, A.mult, 256.0, A.add)
        tt(R("sb"), R("sb"), R("st"), A.add)
        tt(R("sa"), R("sa"), R("sb"), A.add)
        tt(R("sa"), R("sa"), R("cj"), A.max)
        cp(R("so"), R("sa"))
        if t == 0:
            later_constants()
        else:
            act(R("slr"), R("tb"), F.Copy, off=R("so"))
            dma("y", T.sl[:], T.slr[0:128:16, :], (), [R("slr")])
        lands("adh%d" % t, 16, [R("whc%d" % t, 128, 192), R("whs%d" % t, 128, 192)])
        lands("aoh%d" % t, 32, [R("lhc%d" % t), R("lhs%d" % t)])
        for k in BACK.split():
            b = int(k[1])
            pb, src, at, old, to = ("pr", "wh", 64, "b02", 384) if k[0] == "a" else ("pd", "lh", 0, "b13", 256)
            unpack(pb, "f", src + "c%d" % t, src + "s%d" % t, at, b)
            tt(R("xp", 512 * b + to, 512 * b + to + 128), bank(pb, b), R(old, b, 512, 4), A.add)
        X2 = "xi%d" % (t + 1)
        for q, b, lo, hi in PICKS:
            if q != "q":
                pick(q, R(X2, b + 64 * lo, 64 * hi, 4), R("xp", 512 * b, 512 * b + 512), R("so", lo, hi))
                continue
            qn, sn = R("qx%d" % (t + 1), 16 * lo, 16 * hi), R("sx%d" % (t + 1), 16 * lo, 16 * hi)
            quant(qn, sn, R(X2, 64 * lo, 64 * hi))
            if t == 1:
                mm(bank("pr", b), R("qv"), R("sv"), qn, sn)
            elif b == 1:
                mm(bank("pd", 0), R("qu2", 0, 128), R("su2", 0, 128), qn, sn)
    dma("y", T.oc[:], ap(R("qx2")).bitcast(dt.uint8), (), [R("qx2")])
    for k in range(4):
        dma("s" if k % 2 else "y", T.osc[4 * k:4 * k + 4, :], T.sx2[32 * k:32 * k + 4, :], (), [R("sx2")])
    for h in (1, 0):
        cp(R("ycp", 128 * h, 128 * h + 128), bank("pr", h))
    dma("s", T.y[:], ap(R("ycp")), (), [R("ycp")])
    tot["loc"] = nloc[0]
    for sem in sorted(tot):
        wait("g", sem, tot[sem])
